import numpy as np
import ml_dtypes


def mxq(x, axis, fmt="e4m3"):
    dtype, down = {"e4m3": (ml_dtypes.float8_e4m3fn, 7), "e5m2": (ml_dtypes.float8_e5m2, 14)}[fmt]
    v = np.moveaxis(np.asarray(x, np.float32).astype(ml_dtypes.bfloat16).astype(np.float64), axis, -1)
    blocks = v.reshape(v.shape[:-1] + (-1, 32))
    amax = np.abs(blocks).max(-1, keepdims=True)
    byte = np.maximum(np.where(amax > 0, np.frexp(amax)[1] - 1 + 127, 0) - down, 1)
    scale = np.exp2(byte - 127.0)
    codes = (blocks / scale).astype(np.float32).astype(dtype).astype(np.float64)
    return np.moveaxis((codes * scale).reshape(v.shape), -1, axis)


WIDE = False


def mx_kscale(k):
    if not WIDE:
        return np.ones(k)
    levels = np.array([10, -10, 5, -5, 0])
    if k % 512:
        return np.exp2(np.random.permutation(np.resize(levels, k // 32))).repeat(32)
    a = np.empty((k // 512, 16))
    for p in range(k // 512):
        a[p, :8] = np.random.permutation(np.resize(levels, 8))
        for g in range(8):
            far = levels[np.abs(levels - a[p, g]) >= 10]
            a[p, g + 8] = far[np.random.randint(len(far))]
    return np.exp2(a.ravel()).repeat(32)


BF16 = ml_dtypes.bfloat16


def bf(x):
    return np.asarray(x, np.float32).astype(BF16)


def f64(x):
    return np.asarray(x).astype(np.float64)


E2M1 = np.array([0.0, 0.5, 1.0, 1.5, 2.0, 3.0, 4.0, 6.0, -0.0, -0.5, -1.0, -1.5, -2.0, -3.0, -4.0, -6.0])


def pack_weight(w, fmt):
    k, n = w.shape
    w = f64(bf(w)).reshape(k // 32, 32, n)
    amax = np.abs(w).max(1)
    if fmt == "e4m3":
        byte = np.frexp(amax)[1] - 1 + 127 - 7
    else:
        mant, ex = np.frexp(amax / 6.0)
        byte = np.where(mant > 0.5, ex, ex - 1) + 127
    byte = np.clip(np.where(amax > 0, byte, 1), 1, 254)
    scaled = (w * np.exp2(127.0 - byte)[:, None, :]).reshape(k, n).astype(np.float32)
    by_word = np.ascontiguousarray(scaled.reshape(k // 512, 128, 4, n).transpose(0, 1, 3, 2))
    if fmt == "e4m3":
        words = by_word.astype(ml_dtypes.float8_e4m3fn).view(np.uint8)
    else:
        c = by_word.astype(ml_dtypes.float4_e2m1fn).view(np.uint8) & 0xF
        words = c[..., 0::2] | (c[..., 1::2] << 4)
    return np.ascontiguousarray(words), np.ascontiguousarray(byte.astype(np.uint8).reshape(k // 512, 16, n))


def unpack_weight(words, scales, fmt):
    g, p, n, _ = words.shape
    if fmt == "e4m3":
        vals = np.ascontiguousarray(words).view(ml_dtypes.float8_e4m3fn).astype(np.float64)
    else:
        nib = np.empty((g, p, n, 4), np.uint8)
        nib[..., 0::2] = words & 0xF
        nib[..., 1::2] = words >> 4
        vals = E2M1[nib]
    vals = vals * np.repeat(np.exp2(scales.astype(np.float64) - 127.0), 8, axis=1)[..., None]
    return vals.transpose(0, 1, 3, 2).reshape(g * 512, n)
def pack4(w):
    words, scales = pack_weight(w, "e2m1")
    return words.reshape(words.shape[0], 128, -1), scales


def unpack4(words, scales):
    return unpack_weight(words.reshape(words.shape[0], 128, -1, 2), scales, "e2m1")


T, O, I, R = 1024, 1024, 2048, 512

BETA1, BETA2 = 0.8, 0.9


def silu(z):
    return z / (1.0 + np.exp(-z))


def draw0():
    s, t = mx_kscale(T), mx_kscale(I)
    words, scales = pack4(np.random.standard_normal((I, R)) / np.sqrt(I) / t[:, None])
    return {"x": bf(np.random.standard_normal((T, I)) * s[:, None]),
            "dh": bf(2.0 * np.random.standard_normal((T, O)) / np.sqrt(T) / s[:, None]),
            "gate": bf(np.random.standard_normal((T, O))),
            "acc": bf(np.random.standard_normal((O, I))),
            "limit": bf(1.5 * np.exp(0.3 * np.random.standard_normal(O))),
            "precond": bf(np.exp(0.3 * np.random.standard_normal(I)) * t),
            "proj_words": words,
            "proj_scales": scales,
            "m": bf(0.5 * np.random.standard_normal((O, R))),
            "v": bf(0.5 + 0.5 * np.random.standard_normal((O, R)) ** 2)}


def core(x, dh, gate, acc, limit, precond, proj_words, proj_scales, m, v):
    d = f64(dh) * silu(f64(gate))
    grad = f64(acc) + (mxq(d, 0, "e4m3").T @ mxq(f64(x), 0, "e4m3"))
    rms = np.sqrt((grad * grad).mean(axis=1, keepdims=True))
    clip = np.minimum(1.0, f64(limit)[:, None] / rms)
    c = grad * clip * f64(precond)[None, :]
    low = mxq(c, 1, "e4m3") @ unpack4(proj_words, proj_scales)
    m_new = BETA1 * f64(m) + (1.0 - BETA1) * low
    v_new = BETA2 * f64(v) + (1.0 - BETA2) * low * low
    step = m_new / np.sqrt(v_new)
    return m_new, v_new, step


def e4m3fn_bytes(y):
    return np.clip(np.asarray(y, np.float64), -448.0, 448.0).astype(np.float32).astype(ml_dtypes.float8_e4m3fn).view(np.uint8)


def e4m3fn_values(b):
    return np.asarray(b, np.uint8).view(ml_dtypes.float8_e4m3fn).astype(np.float64)


def setup_inputs():
    d = draw0()
    x0 = np.asarray(d['x']).astype(np.float64)
    s = (np.max(np.abs(x0), axis=(1,), keepdims=True) / 448.0).astype(np.float32)
    out = {}
    for k, v in d.items():
        if k == 'x':
            out['x_bytes'] = e4m3fn_bytes(x0 / s.astype(np.float64))
            out['x_scale'] = s
        else:
            out[k] = v
    return out


def reference(x_bytes, x_scale, dh, gate, acc, limit, precond, proj_words, proj_scales, m, v):
    return core(e4m3fn_values(x_bytes) * x_scale.astype(np.float64), dh, gate, acc, limit, precond, proj_words, proj_scales, m, v)

@@ -1,0 +1,245 @@
+from contextlib import ExitStack
+from math import sqrt
+
+import concourse.mybir as mybir
+from concourse.masks import make_identity
+
+T, O, I, R = 1024, 1024, 2048, 512
+FLOPS = 2 * T * O * I + 2 * O * I * R
+
+F32 = mybir.dt.float32
+BF16 = mybir.dt.bfloat16
+I32 = mybir.dt.int32
+U32 = mybir.dt.uint32
+U8 = mybir.dt.uint8
+E4M3FN = mybir.dt.float8_e4m3fn
+FP8X4 = mybir.dt.float8_e4m3fn_x4
+FP4X4 = mybir.dt.float4_e2m1fn_x4
+ACT = mybir.ActivationFunctionType
+ALU = mybir.AluOpType
+
+P = 128
+NB = O // P
+NG1 = T // 512
+NG2 = I // 512
+VECTOR_WIDEN = ((0, 0),)
+AHEAD = 2
+
+
+def tile_galore_up_projection_f1_kernel(tc, x_bytes, x_scale, dh, gate, acc, limit, precond, proj_words, proj_scales, m, v, out_0, out_1, out_2):
+    nc = tc.nc
+    with ExitStack() as ctx:
+        keep = ctx.enter_context(tc.tile_pool(name="keep", bufs=1))
+        stream = ctx.enter_context(tc.tile_pool(name="stream", bufs=12))
+        work = ctx.enter_context(tc.tile_pool(name="work", bufs=2))
+        ps_a = ctx.enter_context(tc.psum_pool(name="ps_a", bufs=4))
+        ps_t = ctx.enter_context(tc.psum_pool(name="ps_t", bufs=2))
+        ps_l = ctx.enter_context(tc.psum_pool(name="ps_l", bufs=2))
+
+        warm = keep.tile([P, 1], F32, name="warm")
+        nc.vector.memset(warm[:], 0.0)
+        nc.scalar.activation(out=warm[:], in_=warm[:], func=ACT.Silu)
+        ident = keep.tile([P, P], F32, name="ident")
+        make_identity(nc, ident[:])
+        lim_rows = keep.tile([P, P], BF16, name="lim_rows")
+        nc.gpsimd.memset(lim_rows[:], 0.0)
+        planes = keep.tile([P, NG2, R], U8, name="planes", align_bytes=64)
+        nc.gpsimd.memset(planes[:].rearrange("p g n -> p (g n)").bitcast(I32), 0)
+
+        xs = keep.tile([P, NG1, 4], F32, name="xs")
+        nc.scalar.dma_start(out=xs[:], in_=x_scale.rearrange("(g p t) o -> p g (t o)", p=P, t=4))
+        x_view = x_bytes.rearrange("(g p t) n -> g p t n", p=P, t=4)
+        gate_view = gate.rearrange("(g p t) n -> g p t n", p=P, t=4)
+        dh_view = dh.rearrange("(g p t) n -> g p t n", p=P, t=4)
+        xb = {}
+        gt = {}
+        dt = {}
+        at = {}
+
+        def load_x(g, c):
+            t_x = keep.tile([P, 4, 1024], U8, name="xb%d%d" % (g, c))
+            nc.sync.dma_start(out=t_x[:], in_=x_view[g][:, :, 1024 * c : 1024 * c + 1024])
+            xb[g, c] = t_x
+
+        def load_gate(g, h):
+            t_g = stream.tile([P, 4, 512], BF16, name="t_g", tag="stream")
+            nc.sync.dma_start(out=t_g[:], in_=gate_view[g][:, :, 512 * h : 512 * h + 512])
+            gt[g, h] = t_g
+
+        def load_dh(g, h):
+            t_d = stream.tile([P, 4, 512], BF16, name="t_d", tag="stream")
+            nc.sync.dma_start(out=t_d[:], in_=dh_view[g][:, :, 512 * h : 512 * h + 512])
+            dt[g, h] = t_d
+
+        def load_acc(b):
+            t_a = stream.tile([P, I], BF16, name="t_a", tag="stream")
+            nc.sync.dma_start(out=t_a[:], in_=acc[P * b : P * b + P, :])
+            at[b] = t_a
+
+        load_x(0, 0)
+        load_gate(0, 0)
+        load_x(1, 0)
+        load_gate(1, 0)
+        load_dh(0, 0)
+        load_dh(1, 0)
+        load_acc(0)
+        load_x(0, 1)
+        load_x(1, 1)
+        load_acc(1)
+        load_gate(0, 1)
+        load_gate(1, 1)
+        load_dh(0, 1)
+        load_dh(1, 1)
+        nc.sync.dma_start(out=lim_rows[0:NB, :], in_=limit.rearrange("(b p) -> b p", p=P))
+        pc = keep.tile([P, I], BF16, name="pc")
+        nc.sync.dma_start(out=pc[:], in_=precond.partition_broadcast(P))
+        load_acc(2)
+        load_acc(3)
+        words = keep.tile([P, NG2, 2 * R], U8, name="words", align_bytes=64)
+        nc.sync.dma_start(out=words[:], in_=proj_words.rearrange("g p n -> p g n"))
+        for q in range(4):
+            nc.sync.dma_start(out=planes[32 * q : 32 * q + 4, :, :].bitcast(I32), in_=proj_scales[:, 4 * q : 4 * q + 4, :].rearrange("g q n -> q g n").bitcast(I32))
+        mt = keep.tile([P, NB, R], BF16, name="mt")
+        vt = keep.tile([P, NB, R], BF16, name="vt")
+        m_view = m.rearrange("(b p) r -> p b r", p=P)
+        v_view = v.rearrange("(b p) r -> p b r", p=P)
+        for s in range(2):
+            nc.sync.dma_start(out=mt[:, 4 * s : 4 * s + 4, :], in_=m_view[:, 4 * s : 4 * s + 4, :])
+            nc.sync.dma_start(out=vt[:, 4 * s : 4 * s + 4, :], in_=v_view[:, 4 * s : 4 * s + 4, :])
+        for b in range(4, NB):
+            load_acc(b)
+
+        d_codes = keep.tile([P, NG1, O], U32, name="d_codes", align_bytes=64)
+        d_scales = keep.tile([P, NG1, O], U8, name="d_scales", align_bytes=64)
+        x_codes = keep.tile([P, NG1, I], U32, name="x_codes", align_bytes=64)
+        x_scales = keep.tile([P, NG1, I], U8, name="x_scales", align_bytes=64)
+
+        def do_d(g, q):
+            cols = slice(256 * (q % 2), 256 * (q % 2) + 256)
+            t_s = work.tile([P, 4, 256], F32, name="t_s")
+            nc.scalar.activation(out=t_s[:], in_=gt[g, q // 2][:, :, cols], func=ACT.Silu)
+            t_di = work.tile([P, 256, 4], BF16, name="t_di", align_bytes=64)
+            nc.vector.tensor_tensor(out=t_di[:], in0=t_s[:].rearrange("p t n -> p n t"), in1=dt[g, q // 2][:, :, cols].rearrange("p t n -> p n t"), op=ALU.mult)
+            o_cols = slice(256 * q, 256 * q + 256)
+            nc.vector.quantize_mx(out=d_codes[:, g, o_cols].bitcast(FP8X4), scales=d_scales[:, g, o_cols], in_=t_di[:].rearrange("p n t -> p (n t)"))
+
+        def do_x(g, j):
+            raw = xb[g, j // 2]
+            c0 = 512 * (j % 2)
+            t_w = work.tile([P, 4, 512], BF16, name="t_w")
+            for t in range(4):
+                src = raw[:, t, c0 : c0 + 512].bitcast(E4M3FN)
+                if (g, j) in VECTOR_WIDEN:
+                    nc.vector.tensor_scalar(out=t_w[:, t, :], in0=src, scalar1=xs[:, g, t : t + 1], scalar2=None, op0=ALU.mult)
+                else:
+                    nc.scalar.activation(out=t_w[:, t, :], in_=src, func=ACT.Copy, scale=xs[:, g, t : t + 1])
+            t_xi = work.tile([P, 512, 4], BF16, name="t_xi", align_bytes=64)
+            nc.vector.tensor_copy(out=t_xi[:], in_=t_w[:].rearrange("p t n -> p n t"))
+            i_cols = slice(512 * j, 512 * j + 512)
+            nc.vector.quantize_mx(out=x_codes[:, g, i_cols].bitcast(FP8X4), scales=x_scales[:, g, i_cols], in_=t_xi[:].rearrange("p n t -> p (n t)"))
+
+        grad = {}
+        ss = {}
+
+        def do_a(b, j):
+            acc_ps = ps_a.tile([P, 512], F32, name="acc_ps")
+            for g in range(NG1):
+                nc.tensor.matmul_mx(
+                    out=acc_ps[:],
+                    lhsT=d_codes[:, g, P * b : P * b + P].bitcast(FP8X4),
+                    lhsT_scale=d_scales[:, g, P * b : P * b + P],
+                    rhs=x_codes[:, g, 512 * j : 512 * j + 512].bitcast(FP8X4),
+                    rhs_scale=x_scales[:, g, 512 * j : 512 * j + 512],
+                    start=(g == 0),
+                    stop=(g == NG1 - 1),
+                )
+            if j == 0:
+                t_grad = work.tile([P, I], F32, name="t_grad", bufs=4)
+                grad[b] = t_grad
+                t_ss = work.tile([P, 2], F32, name="t_ss", bufs=4)
+                ss[b] = t_ss
+            nc.vector.tensor_tensor(out=grad[b][:, 512 * j : 512 * j + 512], in0=acc_ps[:], in1=at[b][:, 512 * j : 512 * j + 512], op=ALU.add)
+            if j % 2 == 1:
+                h = j // 2
+                junk = work.tile([P, 1024], BF16, name="junk", bufs=1)
+                nc.scalar.activation(out=junk[:], in_=grad[b][:, 1024 * h : 1024 * h + 1024], func=ACT.Square, accum_out=ss[b][:, h : h + 1])
+
+        lim = keep.tile([P, NB], F32, name="lim")
+
+        def do_limit():
+            lim32 = keep.tile([P, P], F32, name="lim32")
+            nc.vector.tensor_copy(out=lim32[:], in_=lim_rows[:])
+            lim_ps = ps_t.tile([P, P], F32, name="lim_ps", tag="ps_t")
+            nc.tensor.transpose(lim_ps[:], lim32[:], ident[:])
+            nc.vector.tensor_scalar(out=lim[:], in0=lim_ps[:, 0:NB], scalar1=sqrt(float(I)), scalar2=None, op0=ALU.mult)
+
+        c_codes = {}
+
+        def do_c(b):
+            t_r = work.tile([P, 1], F32, name="t_r")
+            nc.scalar.activation(out=t_r[:], in_=ss[b][:, 0:1], func=ACT.Abs_reciprocal_sqrt, bias=ss[b][:, 1:2])
+            t_clip = work.tile([P, 1], F32, name="t_clip")
+            nc.vector.tensor_scalar(out=t_clip[:], in0=t_r[:], scalar1=lim[:, b : b + 1], scalar2=1.0, op0=ALU.mult, op1=ALU.min)
+            t_c = work.tile([P, I], BF16, name="t_c")
+            t_ct = work.tile([P, NG2, P, 4], BF16, name="t_ct", align_bytes=64)
+            for h in range(2):
+                cols = slice(1024 * h, 1024 * h + 1024)
+                nc.vector.scalar_tensor_tensor(out=t_c[:, cols], in0=grad[b][:, cols], scalar=t_clip[:], in1=pc[:, cols], op0=ALU.mult, op1=ALU.mult)
+                ct_ps = ps_t.tile([P, 2, 2, P], F32, name="ct_ps", tag="ps_t")
+                pairs = t_c[:].bitcast(F32)
+                for k in range(2):
+                    for u in range(2):
+                        base = 256 * (2 * h + k)
+                        nc.tensor.transpose(ct_ps[:, k, u, :], pairs[:, base + u : base + 256 : 2], ident[:])
+                nc.scalar.copy(out=t_ct[:, 2 * h : 2 * h + 2, :, :].rearrange("p g o t -> p g (o t)").bitcast(F32).rearrange("p g (o u) -> p g o u", u=2), in_=ct_ps[:].rearrange("p k u o -> p k o u"))
+            t_cq = work.tile([P, NG2 * P], U32, name="t_cq", align_bytes=64)
+            t_cs = work.tile([P, NG2 * P], U8, name="t_cs", align_bytes=64)
+            nc.vector.quantize_mx(out=t_cq[:].bitcast(FP8X4), scales=t_cs[:], in_=t_ct[:].rearrange("p g o t -> p (g o t)"))
+            c_codes[b] = (t_cq, t_cs)
+
+        def do_low(b):
+            t_cq, t_cs = c_codes[b]
+            low = ps_l.tile([P, R], F32, name="low")
+            for g in range(NG2):
+                nc.tensor.matmul_mx(
+                    out=low[:],
+                    lhsT=t_cq[:, P * g : P * g + P].bitcast(FP8X4),
+                    lhsT_scale=t_cs[:, P * g : P * g + P],
+                    rhs=words[:, g, :].bitcast(FP4X4),
+                    rhs_scale=planes[:, g, :],
+                    start=(g == 0),
+                    stop=(g == NG2 - 1),
+                )
+            rows = slice(P * b, P * b + P)
+            t_sq = work.tile([P, R], F32, name="t_sq")
+            nc.scalar.activation(out=t_sq[:], in_=low[:], func=ACT.Square, scale=sqrt(0.1))
+            t_m = work.tile([P, R], F32, name="t_m")
+            nc.vector.scalar_tensor_tensor(out=t_m[:], in0=low[:], scalar=0.25, in1=mt[:, b, :], op0=ALU.mult, op1=ALU.add)
+            t_v = work.tile([P, R], F32, name="t_v")
+            nc.vector.scalar_tensor_tensor(out=t_v[:], in0=vt[:, b, :], scalar=0.9, in1=t_sq[:], op0=ALU.mult, op1=ALU.add)
+            nc.sync.dma_start(out=out_1[rows, :], in_=t_v[:])
+            t_mn = work.tile([P, R], F32, name="t_mn")
+            nc.scalar.activation(out=t_mn[:], in_=t_m[:], func=ACT.Copy, scale=0.8)
+            nc.sync.dma_start(out=out_0[rows, :], in_=t_mn[:])
+            t_rs = work.tile([P, R], F32, name="t_rs")
+            nc.scalar.activation(out=t_rs[:], in_=t_v[:], func=ACT.Abs_reciprocal_sqrt, scale=1.0 / 0.64)
+            t_st = work.tile([P, R], F32, name="t_st")
+            nc.vector.tensor_tensor(out=t_st[:], in0=t_m[:], in1=t_rs[:], op=ALU.mult)
+            nc.sync.dma_start(out=out_2[rows, :], in_=t_st[:])
+
+        for j in range(4):
+            for g in range(NG1):
+                do_x(g, j)
+            for g in range(NG1):
+                do_d(g, j)
+            for b in range(AHEAD):
+                do_a(b, j)
+        do_limit()
+        for b in range(NB):
+            if b + AHEAD < NB:
+                for j in range(4):
+                    do_a(b + AHEAD, j)
+            do_c(b)
+            if b > 0:
+                do_low(b - 1)
+        do_low(NB - 1)

@@ -23,22 +23,34 @@ NB = O // P
 NG1 = T // 512
 NG2 = I // 512
 VECTOR_WIDEN = ((0, 0),)
-AHEAD = 2
+SCALAR_INTER = ((0, 3),(1, 3))
+G_DMUL = ((0, 2), (1, 2), (0, 3), (1, 3))
+G_EPI = 7
+SEQ = (("load_x", 0, 0,), ("widen", 0, 0,), ("load_gate", 0, 0,), ("inter", 0, 0,), ("load_x", 1, 0,), ("load_dh", 0, 0,), ("load_gate", 1, 0,), ("silu", 0, 0,), ("widen", 1, 0,), ("xq", 0, 0,), ("dmul", 0, 0,), ("inter", 1, 0,), ("silu", 1, 0,), ("load_dh", 1, 0,), ("silu", 0, 1,), ("dq", 0, 0,), ("load_acc", 0,), ("dmul", 1, 0,), ("dmul", 0, 1,), ("dq", 0, 1,), ("dq", 1, 0,), ("xq", 1, 0,), ("amm", 0, 0,), ("widen", 0, 1,), ("inter", 0, 1,), ("silu", 1, 1,), ("dmul", 1, 1,), ("widen", 1, 1,), ("xq", 0, 1,), ("load_gate", 1, 1,), ("inter", 1, 1,), ("load_x", 0, 1,), ("widen", 0, 2,), ("inter", 0, 2,), ("load_dh", 0, 1,), ("xq", 1, 1,), ("amm", 0, 1,), ("load_gate", 0, 1,), ("silu", 0, 2,), ("load_acc", 7,), ("load_x", 1, 1,), ("add", 0, 0,), ("add", 0, 1,), ("dmul", 0, 2,), ("silu", 1, 2,), ("widen", 1, 2,), ("inter", 1, 2,), ("dq", 1, 1,), ("load_acc", 3,), ("widen", 1, 3,), ("load_acc", 1,), ("xq", 0, 2,), ("xq", 1, 2,), ("load_dh", 1, 1,), ("widen", 0, 3,), ("amm", 1, 0,), ("amm", 1, 1,), ("add", 1, 0,), ("inter", 1, 3,), ("amm", 0, 2,), ("inter", 0, 3,), ("load_acc", 2,), ("add", 1, 1,), ("load_acc", 4,), ("amm", 2, 0,), ("add", 0, 2,), ("late", 1,), ("add", 2, 0,), ("late", 3,), ("dmul", 1, 2,), ("dq", 0, 2,), ("amm", 2, 1,), ("amm", 1, 2,), ("xq", 1, 3,), ("xq", 0, 3,), ("amm", 0, 3,), ("add", 2, 1,), ("add", 0, 3,), ("late", 0,), ("amm", 2, 3,), ("vectors",), ("dq", 1, 2,), ("silu", 1, 3,), ("silu", 0, 3,), ("late", 4,), ("add", 1, 2,), ("add", 2, 3,), ("sqr", 0,), ("amm", 1, 3,), ("ars", 0,), ("late", 2,), ("amm", 2, 2,), ("add", 1, 3,), ("sqr", 1,), ("add", 2, 2,), ("amm", 3, 0,), ("dmul", 1, 3,), ("ars", 1,), ("dq", 1, 3,), ("clip", 0,), ("cmul", 0, 0,), ("cmul", 0, 1,), ("amm", 3, 2,), ("clip", 1,), ("tr", 0, 0,), ("add", 3, 0,), ("cpt", 0, 0,), ("tr", 0, 1,), ("cmul", 1, 0,), ("cpt", 0, 1,), ("load_acc", 6,), ("amm", 3, 1,), ("load_acc", 5,), ("cq", 0,), ("add", 3, 2,), ("dmul", 0, 3,), ("ev9", 0,), ("tr", 1, 0,), ("lmm", 0,), ("amm", 3, 3,), ("sqr", 2,), ("ars", 2,), ("cmul", 1, 1,), ("add", 3, 1,), ("tr", 1, 1,), ("em", 0,), ("cpt", 1, 0,), ("cpt", 1, 1,), ("amm", 4, 0,), ("amm", 5, 0,), ("clip", 2,), ("esq", 0,), ("emn", 0,), ("ev9", 7,), ("ev", 0,), ("add", 3, 3,), ("cmul", 2, 0,), ("sqr", 3,), ("ars", 3,), ("amm", 4, 1,), ("add", 4, 0,), ("add", 5, 0,), ("add", 4, 1,), ("cq", 1,), ("tr", 2, 0,), ("amm", 4, 2,), ("add", 4, 2,), ("cmul", 2, 1,), ("clip", 3,), ("amm", 5, 1,), ("add", 5, 1,), ("lmm", 1,), ("ev9", 1,), ("amm", 4, 3,), ("tr", 2, 1,), ("add", 4, 3,), ("cpt", 2, 0,), ("amm", 5, 2,), ("ers", 0,), ("esq", 1,), ("cpt", 2, 1,), ("amm", 5, 3,), ("est", 0,), ("em", 1,), ("cmul", 3, 0,), ("tr", 3, 0,), ("ev", 1,), ("cq", 2,), ("add", 5, 2,), ("sqr", 4,), ("lmm", 2,), ("ev9", 2,), ("dq", 0, 3,), ("cmul", 3, 1,), ("add", 5, 3,), ("emn", 1,), ("amm", 6, 0,), ("amm", 6, 1,), ("ers", 1,), ("add", 6, 0,), ("ars", 4,), ("clip", 4,), ("add", 6, 1,), ("cmul", 4, 0,), ("esq", 2,), ("cpt", 3, 0,), ("amm", 6, 3,), ("ev", 2,), ("sqr", 5,), ("tr", 3, 1,), ("amm", 6, 2,), ("cpt", 3, 1,), ("amm", 7, 0,), ("ers", 2,), ("add", 6, 3,), ("add", 6, 2,), ("ars", 5,), ("tr", 4, 0,), ("cq", 3,), ("sqr", 6,), ("amm", 7, 3,), ("em", 2,), ("clip", 5,), ("amm", 7, 1,), ("lmm", 3,), ("esq", 3,), ("add", 7, 0,), ("est", 1,), ("cmul", 4, 1,), ("amm", 7, 2,), ("tr", 4, 1,), ("em", 3,), ("add", 7, 1,), ("add", 7, 2,), ("ev9", 3,), ("ars", 6,), ("cpt", 4, 0,), ("cpt", 4, 1,), ("emn", 2,), ("est", 2,), ("add", 7, 3,), ("ev", 3,), ("cq", 4,), ("cmul", 5, 0,), ("ev9", 4,), ("clip", 6,), ("ers", 3,), ("est", 3,), ("sqr", 7,), ("lmm", 4,), ("cmul", 5, 1,), ("esq", 4,), ("emn", 3,), ("tr", 5, 0,), ("ars", 7,), ("tr", 5, 1,), ("cmul", 6, 0,), ("cpt", 5, 0,), ("ev", 4,), ("cpt", 5, 1,), ("em", 4,), ("cq", 5,), ("ers", 4,), ("est", 4,), ("tr", 6, 0,), ("clip", 7,), ("lmm", 5,), ("esq", 5,), ("cpt", 6, 0,), ("ev9", 5,), ("cmul", 6, 1,), ("em", 5,), ("tr", 6, 1,), ("cmul", 7, 0,), ("tr", 7, 0,), ("cpt", 6, 1,), ("cpt", 7, 0,), ("ev", 5,), ("cq", 6,), ("emn", 5,), ("cmul", 7, 1,), ("lmm", 6,), ("ers", 5,), ("tr", 7, 1,), ("emn", 4,), ("em", 6,), ("cpt", 7, 1,), ("ev9", 6,), ("est", 5,), ("esq", 6,), ("cq", 7,), ("lmm", 7,), ("esq", 7,), ("ev", 6,), ("ers", 6,), ("em", 7,), ("emn", 6,), ("ev", 7,), ("emn", 7,), ("ers", 7,), ("est", 6,), ("est", 7,))
+GRADS = 5
 
 
 def tile_galore_up_projection_f1_kernel(tc, x_bytes, x_scale, dh, gate, acc, limit, precond, proj_words, proj_scales, m, v, out_0, out_1, out_2):
     nc = tc.nc
     with ExitStack() as ctx:
         keep = ctx.enter_context(tc.tile_pool(name="keep", bufs=1))
-        stream = ctx.enter_context(tc.tile_pool(name="stream", bufs=12))
+        stream = ctx.enter_context(tc.tile_pool(name="stream", bufs=10))
         work = ctx.enter_context(tc.tile_pool(name="work", bufs=2))
-        ps_a = ctx.enter_context(tc.psum_pool(name="ps_a", bufs=4))
+        ps_p = ctx.enter_context(tc.psum_pool(name="ps_p", bufs=1))
+        ps_a = ctx.enter_context(tc.psum_pool(name="ps_a", bufs=3))
         ps_t = ctx.enter_context(tc.psum_pool(name="ps_t", bufs=2))
-        ps_l = ctx.enter_context(tc.psum_pool(name="ps_l", bufs=2))
+        ps_l = ctx.enter_context(tc.psum_pool(name="ps_l", bufs=1))
+        ctx.enter_context(tc.manual_schedule())
 
         warm = keep.tile([P, 1], F32, name="warm")
         nc.vector.memset(warm[:], 0.0)
         nc.scalar.activation(out=warm[:], in_=warm[:], func=ACT.Silu)
+        xs = keep.tile([P, NG1, 4], F32, name="xs")
+        nc.sync.dma_start(out=xs[:], in_=x_scale.rearrange("(g p t) o -> p g (t o)", p=P, t=4))
+        pc_rows = keep.tile([P, I], BF16, name="pc_rows")
+        nc.gpsimd.memset(pc_rows[:].bitcast(I32), 0)
+        ones = keep.tile([P, P], BF16, name="ones")
+        nc.gpsimd.memset(ones[:], 1.0)
         ident = keep.tile([P, P], F32, name="ident")
         make_identity(nc, ident[:])
         lim_rows = keep.tile([P, P], BF16, name="lim_rows")
@@ -46,8 +58,6 @@ def tile_galore_up_projection_f1_kernel(tc, x_bytes, x_scale, dh, gate, acc, lim
         planes = keep.tile([P, NG2, R], U8, name="planes", align_bytes=64)
         nc.gpsimd.memset(planes[:].rearrange("p g n -> p (g n)").bitcast(I32), 0)
 
-        xs = keep.tile([P, NG1, 4], F32, name="xs")
-        nc.scalar.dma_start(out=xs[:], in_=x_scale.rearrange("(g p t) o -> p g (t o)", p=P, t=4))
         x_view = x_bytes.rearrange("(g p t) n -> g p t n", p=P, t=4)
         gate_view = gate.rearrange("(g p t) n -> g p t n", p=P, t=4)
         dh_view = dh.rearrange("(g p t) n -> g p t n", p=P, t=4)
@@ -76,72 +86,73 @@ def tile_galore_up_projection_f1_kernel(tc, x_bytes, x_scale, dh, gate, acc, lim
             nc.sync.dma_start(out=t_a[:], in_=acc[P * b : P * b + P, :])
             at[b] = t_a
 
-        load_x(0, 0)
-        load_gate(0, 0)
-        load_x(1, 0)
-        load_gate(1, 0)
-        load_dh(0, 0)
-        load_dh(1, 0)
-        load_acc(0)
-        load_x(0, 1)
-        load_x(1, 1)
-        load_acc(1)
-        load_gate(0, 1)
-        load_gate(1, 1)
-        load_dh(0, 1)
-        load_dh(1, 1)
-        nc.sync.dma_start(out=lim_rows[0:NB, :], in_=limit.rearrange("(b p) -> b p", p=P))
-        pc = keep.tile([P, I], BF16, name="pc")
-        nc.sync.dma_start(out=pc[:], in_=precond.partition_broadcast(P))
-        load_acc(2)
-        load_acc(3)
-        words = keep.tile([P, NG2, 2 * R], U8, name="words", align_bytes=64)
-        nc.sync.dma_start(out=words[:], in_=proj_words.rearrange("g p n -> p g n"))
-        for q in range(4):
-            nc.sync.dma_start(out=planes[32 * q : 32 * q + 4, :, :].bitcast(I32), in_=proj_scales[:, 4 * q : 4 * q + 4, :].rearrange("g q n -> q g n").bitcast(I32))
-        mt = keep.tile([P, NB, R], BF16, name="mt")
-        vt = keep.tile([P, NB, R], BF16, name="vt")
-        m_view = m.rearrange("(b p) r -> p b r", p=P)
-        v_view = v.rearrange("(b p) r -> p b r", p=P)
-        for s in range(2):
-            nc.sync.dma_start(out=mt[:, 4 * s : 4 * s + 4, :], in_=m_view[:, 4 * s : 4 * s + 4, :])
-            nc.sync.dma_start(out=vt[:, 4 * s : 4 * s + 4, :], in_=v_view[:, 4 * s : 4 * s + 4, :])
-        for b in range(4, NB):
-            load_acc(b)
-
         d_codes = keep.tile([P, NG1, O], U32, name="d_codes", align_bytes=64)
         d_scales = keep.tile([P, NG1, O], U8, name="d_scales", align_bytes=64)
         x_codes = keep.tile([P, NG1, I], U32, name="x_codes", align_bytes=64)
         x_scales = keep.tile([P, NG1, I], U8, name="x_scales", align_bytes=64)
+        words = keep.tile([P, NG2, 2 * R], U8, name="words", align_bytes=64)
+        mt = keep.tile([P, NB, R], BF16, name="mt")
+        vt = keep.tile([P, NB, R], BF16, name="vt")
+        m_view = m.rearrange("(b p) r -> p b r", p=P)
+        v_view = v.rearrange("(b p) r -> p b r", p=P)
 
-        def do_d(g, q):
+        ts_ = {}
+        tdi = {}
+        tw = {}
+        txi = {}
+        aps = {}
+        grad = {}
+        ss = {}
+        rr = {}
+        cl = {}
+        tcb = {}
+        tct = {}
+        ctp = {}
+        cqs = {}
+        lows = {}
+        ep = {}
+
+        def silu(g, q):
             cols = slice(256 * (q % 2), 256 * (q % 2) + 256)
-            t_s = work.tile([P, 4, 256], F32, name="t_s")
+            t_s = work.tile([P, 4, 256], F32, name="t_s", bufs=2)
             nc.scalar.activation(out=t_s[:], in_=gt[g, q // 2][:, :, cols], func=ACT.Silu)
-            t_di = work.tile([P, 256, 4], BF16, name="t_di", align_bytes=64)
-            nc.vector.tensor_tensor(out=t_di[:], in0=t_s[:].rearrange("p t n -> p n t"), in1=dt[g, q // 2][:, :, cols].rearrange("p t n -> p n t"), op=ALU.mult)
-            o_cols = slice(256 * q, 256 * q + 256)
-            nc.vector.quantize_mx(out=d_codes[:, g, o_cols].bitcast(FP8X4), scales=d_scales[:, g, o_cols], in_=t_di[:].rearrange("p n t -> p (n t)"))
+            ts_[g, q] = t_s
 
-        def do_x(g, j):
-            raw = xb[g, j // 2]
+        def dmul(g, q):
+            cols = slice(256 * (q % 2), 256 * (q % 2) + 256)
+            t_di = work.tile([P, 256, 4], BF16, name="t_di", align_bytes=64)
+            eng = nc.gpsimd if (g, q) in G_DMUL else nc.vector
+            eng.tensor_tensor(out=t_di[:], in0=ts_[g, q][:].rearrange("p t n -> p n t"), in1=dt[g, q // 2][:, :, cols].rearrange("p t n -> p n t"), op=ALU.mult)
+            tdi[g, q] = t_di
+
+        def dq(g, q):
+            o_cols = slice(256 * q, 256 * q + 256)
+            nc.vector.quantize_mx(out=d_codes[:, g, o_cols].bitcast(FP8X4), scales=d_scales[:, g, o_cols], in_=tdi[g, q][:].rearrange("p n t -> p (n t)"))
+
+        def widen(g, j):
             c0 = 512 * (j % 2)
             t_w = work.tile([P, 4, 512], BF16, name="t_w")
             for t in range(4):
-                src = raw[:, t, c0 : c0 + 512].bitcast(E4M3FN)
+                src = xb[g, j // 2][:, t, c0 : c0 + 512].bitcast(E4M3FN)
                 if (g, j) in VECTOR_WIDEN:
                     nc.vector.tensor_scalar(out=t_w[:, t, :], in0=src, scalar1=xs[:, g, t : t + 1], scalar2=None, op0=ALU.mult)
                 else:
                     nc.scalar.activation(out=t_w[:, t, :], in_=src, func=ACT.Copy, scale=xs[:, g, t : t + 1])
+            tw[g, j] = t_w
+
+        def inter(g, j):
             t_xi = work.tile([P, 512, 4], BF16, name="t_xi", align_bytes=64)
-            nc.vector.tensor_copy(out=t_xi[:], in_=t_w[:].rearrange("p t n -> p n t"))
+            if (g, j) in SCALAR_INTER:
+                nc.scalar.copy(out=t_xi[:], in_=tw[g, j][:].rearrange("p t n -> p n t"))
+            else:
+                nc.vector.tensor_copy(out=t_xi[:], in_=tw[g, j][:].rearrange("p t n -> p n t"))
+            txi[g, j] = t_xi
+
+        def xq(g, j):
             i_cols = slice(512 * j, 512 * j + 512)
-            nc.vector.quantize_mx(out=x_codes[:, g, i_cols].bitcast(FP8X4), scales=x_scales[:, g, i_cols], in_=t_xi[:].rearrange("p n t -> p (n t)"))
+            nc.vector.quantize_mx(out=x_codes[:, g, i_cols].bitcast(FP8X4), scales=x_scales[:, g, i_cols], in_=txi[g, j][:].rearrange("p n t -> p (n t)"))
 
-        grad = {}
-        ss = {}
-
-        def do_a(b, j):
+        def amm(b, j):
             acc_ps = ps_a.tile([P, 512], F32, name="acc_ps")
             for g in range(NG1):
                 nc.tensor.matmul_mx(
@@ -153,52 +164,73 @@ def tile_galore_up_projection_f1_kernel(tc, x_bytes, x_scale, dh, gate, acc, lim
                     start=(g == 0),
                     stop=(g == NG1 - 1),
                 )
+            aps[b, j] = acc_ps
+
+        def add(b, j):
             if j == 0:
-                t_grad = work.tile([P, I], F32, name="t_grad", bufs=4)
+                t_grad = work.tile([P, I], F32, name="t_grad", bufs=GRADS)
                 grad[b] = t_grad
-                t_ss = work.tile([P, 2], F32, name="t_ss", bufs=4)
+                t_ss = work.tile([P, 1], F32, name="t_ss", bufs=GRADS)
                 ss[b] = t_ss
-            nc.vector.tensor_tensor(out=grad[b][:, 512 * j : 512 * j + 512], in0=acc_ps[:], in1=at[b][:, 512 * j : 512 * j + 512], op=ALU.add)
-            if j % 2 == 1:
-                h = j // 2
-                junk = work.tile([P, 1024], BF16, name="junk", bufs=1)
-                nc.scalar.activation(out=junk[:], in_=grad[b][:, 1024 * h : 1024 * h + 1024], func=ACT.Square, accum_out=ss[b][:, h : h + 1])
+            nc.vector.tensor_tensor(out=grad[b][:, 512 * j : 512 * j + 512], in0=aps[b, j][:], in1=at[b][:, 512 * j : 512 * j + 512], op=ALU.add)
+
+        def sqr(b):
+            junk = work.tile([P, I], BF16, name="junk", bufs=1)
+            nc.scalar.activation(out=junk[:], in_=grad[b][:], func=ACT.Square, accum_out=ss[b][:])
 
         lim = keep.tile([P, NB], F32, name="lim")
+        lim32 = keep.tile([P, P], F32, name="lim32")
+        pc = ps_p.tile([P, I], BF16, name="pc")
 
-        def do_limit():
-            lim32 = keep.tile([P, P], F32, name="lim32")
+        def vectors():
             nc.vector.tensor_copy(out=lim32[:], in_=lim_rows[:])
             lim_ps = ps_t.tile([P, P], F32, name="lim_ps", tag="ps_t")
             nc.tensor.transpose(lim_ps[:], lim32[:], ident[:])
-            nc.vector.tensor_scalar(out=lim[:], in0=lim_ps[:, 0:NB], scalar1=sqrt(float(I)), scalar2=None, op0=ALU.mult)
+            nc.vector.tensor_copy(out=lim[:], in_=lim_ps[:, 0:NB])
+            for c in range(4):
+                cols = slice(512 * c, 512 * c + 512)
+                nc.tensor.matmul(pc[:, cols], lhsT=ones[:], rhs=pc_rows[:, cols], start=True, stop=True)
 
-        c_codes = {}
-
-        def do_c(b):
+        def ars(b):
             t_r = work.tile([P, 1], F32, name="t_r")
-            nc.scalar.activation(out=t_r[:], in_=ss[b][:, 0:1], func=ACT.Abs_reciprocal_sqrt, bias=ss[b][:, 1:2])
+            nc.scalar.activation(out=t_r[:], in_=ss[b][:], func=ACT.Abs_reciprocal_sqrt, scale=1.0 / I)
+            rr[b] = t_r
+
+        def clip(b):
             t_clip = work.tile([P, 1], F32, name="t_clip")
-            nc.vector.tensor_scalar(out=t_clip[:], in0=t_r[:], scalar1=lim[:, b : b + 1], scalar2=1.0, op0=ALU.mult, op1=ALU.min)
-            t_c = work.tile([P, I], BF16, name="t_c")
-            t_ct = work.tile([P, NG2, P, 4], BF16, name="t_ct", align_bytes=64)
-            for h in range(2):
-                cols = slice(1024 * h, 1024 * h + 1024)
-                nc.vector.scalar_tensor_tensor(out=t_c[:, cols], in0=grad[b][:, cols], scalar=t_clip[:], in1=pc[:, cols], op0=ALU.mult, op1=ALU.mult)
-                ct_ps = ps_t.tile([P, 2, 2, P], F32, name="ct_ps", tag="ps_t")
-                pairs = t_c[:].bitcast(F32)
-                for k in range(2):
-                    for u in range(2):
-                        base = 256 * (2 * h + k)
-                        nc.tensor.transpose(ct_ps[:, k, u, :], pairs[:, base + u : base + 256 : 2], ident[:])
-                nc.scalar.copy(out=t_ct[:, 2 * h : 2 * h + 2, :, :].rearrange("p g o t -> p g (o t)").bitcast(F32).rearrange("p g (o u) -> p g o u", u=2), in_=ct_ps[:].rearrange("p k u o -> p k o u"))
+            nc.vector.tensor_scalar(out=t_clip[:], in0=rr[b][:], scalar1=lim[:, b : b + 1], scalar2=1.0, op0=ALU.mult, op1=ALU.min)
+            cl[b] = t_clip
+
+        def cmul(b, h):
+            if h == 0:
+                t_c = work.tile([P, I], BF16, name="t_c")
+                tcb[b] = t_c
+            cols = slice(1024 * h, 1024 * h + 1024)
+            nc.vector.scalar_tensor_tensor(out=tcb[b][:, cols], in0=grad[b][:, cols], scalar=cl[b][:], in1=pc[:, cols], op0=ALU.mult, op1=ALU.mult)
+
+        def tr(b, h):
+            ct_ps = ps_t.tile([P, 2, 2, P], F32, name="ct_ps", tag="ps_t")
+            pairs = tcb[b][:].bitcast(F32)
+            for k in range(2):
+                for u in range(2):
+                    base = 256 * (2 * h + k)
+                    nc.tensor.transpose(ct_ps[:, k, u, :], pairs[:, base + u : base + 256 : 2], ident[:])
+            ctp[b, h] = ct_ps
+
+        def cpt(b, h):
+            if h == 0:
+                t_ct = work.tile([P, NG2, P, 4], BF16, name="t_ct", align_bytes=64)
+                tct[b] = t_ct
+            nc.scalar.copy(out=tct[b][:, 2 * h : 2 * h + 2, :, :].rearrange("p g o t -> p g (o t)").bitcast(F32).rearrange("p g (o u) -> p g o u", u=2), in_=ctp[b, h][:].rearrange("p k u o -> p k o u"))
+
+        def cq(b):
             t_cq = work.tile([P, NG2 * P], U32, name="t_cq", align_bytes=64)
             t_cs = work.tile([P, NG2 * P], U8, name="t_cs", align_bytes=64)
-            nc.vector.quantize_mx(out=t_cq[:].bitcast(FP8X4), scales=t_cs[:], in_=t_ct[:].rearrange("p g o t -> p (g o t)"))
-            c_codes[b] = (t_cq, t_cs)
+            nc.vector.quantize_mx(out=t_cq[:].bitcast(FP8X4), scales=t_cs[:], in_=tct[b][:].rearrange("p g o t -> p (g o t)"))
+            cqs[b] = (t_cq, t_cs)
 
-        def do_low(b):
-            t_cq, t_cs = c_codes[b]
+        def lmm(b):
+            t_cq, t_cs = cqs[b]
             low = ps_l.tile([P, R], F32, name="low")
             for g in range(NG2):
                 nc.tensor.matmul_mx(
@@ -210,36 +242,69 @@ def tile_galore_up_projection_f1_kernel(tc, x_bytes, x_scale, dh, gate, acc, lim
                     start=(g == 0),
                     stop=(g == NG2 - 1),
                 )
-            rows = slice(P * b, P * b + P)
-            t_sq = work.tile([P, R], F32, name="t_sq")
-            nc.scalar.activation(out=t_sq[:], in_=low[:], func=ACT.Square, scale=sqrt(0.1))
-            t_m = work.tile([P, R], F32, name="t_m")
-            nc.vector.scalar_tensor_tensor(out=t_m[:], in0=low[:], scalar=0.25, in1=mt[:, b, :], op0=ALU.mult, op1=ALU.add)
-            t_v = work.tile([P, R], F32, name="t_v")
-            nc.vector.scalar_tensor_tensor(out=t_v[:], in0=vt[:, b, :], scalar=0.9, in1=t_sq[:], op0=ALU.mult, op1=ALU.add)
-            nc.sync.dma_start(out=out_1[rows, :], in_=t_v[:])
-            t_mn = work.tile([P, R], F32, name="t_mn")
-            nc.scalar.activation(out=t_mn[:], in_=t_m[:], func=ACT.Copy, scale=0.8)
-            nc.sync.dma_start(out=out_0[rows, :], in_=t_mn[:])
-            t_rs = work.tile([P, R], F32, name="t_rs")
-            nc.scalar.activation(out=t_rs[:], in_=t_v[:], func=ACT.Abs_reciprocal_sqrt, scale=1.0 / 0.64)
-            t_st = work.tile([P, R], F32, name="t_st")
-            nc.vector.tensor_tensor(out=t_st[:], in0=t_m[:], in1=t_rs[:], op=ALU.mult)
-            nc.sync.dma_start(out=out_2[rows, :], in_=t_st[:])
+            lows[b] = low
 
-        for j in range(4):
-            for g in range(NG1):
-                do_x(g, j)
-            for g in range(NG1):
-                do_d(g, j)
-            for b in range(AHEAD):
-                do_a(b, j)
-        do_limit()
-        for b in range(NB):
-            if b + AHEAD < NB:
-                for j in range(4):
-                    do_a(b + AHEAD, j)
-            do_c(b)
-            if b > 0:
-                do_low(b - 1)
-        do_low(NB - 1)
+        def on_g(b):
+            return b < G_EPI
+
+        def esq(b):
+            t_sq = work.tile([P, R], F32, name="t_sq")
+            nc.scalar.activation(out=t_sq[:], in_=lows[b][:], func=ACT.Square, scale=sqrt(0.1))
+            ep[b, "sq"] = t_sq
+
+        def em(b):
+            t_m = work.tile([P, R], F32, name="t_m")
+            nc.vector.scalar_tensor_tensor(out=t_m[:], in0=lows[b][:], scalar=0.25, in1=mt[:, b, :], op0=ALU.mult, op1=ALU.add)
+            ep[b, "m"] = t_m
+
+        def ev9(b):
+            if on_g(b):
+                t_v9 = work.tile([P, R], F32, name="t_v9", bufs=1)
+                nc.gpsimd.tensor_scalar(out=t_v9[:], in0=vt[:, b, :], scalar1=0.9, scalar2=0.0, op0=ALU.mult, op1=ALU.add)
+                ep[b, "v9"] = t_v9
+
+        def ev(b):
+            t_v = work.tile([P, R], F32, name="t_v", bufs=3)
+            if on_g(b):
+                nc.gpsimd.tensor_tensor(out=t_v[:], in0=ep[b, "v9"][:], in1=ep[b, "sq"][:], op=ALU.add)
+            else:
+                nc.vector.scalar_tensor_tensor(out=t_v[:], in0=vt[:, b, :], scalar=0.9, in1=ep[b, "sq"][:], op0=ALU.mult, op1=ALU.add)
+            nc.sync.dma_start(out=out_1[P * b : P * b + P, :], in_=t_v[:])
+            ep[b, "v"] = t_v
+
+        def emn(b):
+            t_mn = work.tile([P, R], F32, name="t_mn", bufs=3)
+            if on_g(b):
+                nc.gpsimd.tensor_scalar(out=t_mn[:], in0=ep[b, "m"][:], scalar1=0.8, scalar2=0.0, op0=ALU.mult, op1=ALU.add)
+            else:
+                nc.scalar.activation(out=t_mn[:], in_=ep[b, "m"][:], func=ACT.Copy, scale=0.8)
+            nc.sync.dma_start(out=out_0[P * b : P * b + P, :], in_=t_mn[:])
+
+        def ers(b):
+            t_rs = work.tile([P, R], F32, name="t_rs", bufs=3)
+            nc.scalar.activation(out=t_rs[:], in_=ep[b, "v"][:], func=ACT.Abs_reciprocal_sqrt, scale=1.0 / 0.64)
+            ep[b, "rs"] = t_rs
+
+        def est(b):
+            t_st = ep[b, "rs"]
+            eng = nc.gpsimd if on_g(b) else nc.vector
+            eng.tensor_tensor(out=t_st[:], in0=ep[b, "m"][:], in1=ep[b, "rs"][:], op=ALU.mult)
+            nc.sync.dma_start(out=out_2[P * b : P * b + P, :], in_=t_st[:])
+
+        def late(k):
+            if k == 0:
+                nc.sync.dma_start(out=pc_rows[0:1, :], in_=precond.rearrange("(o n) -> o n", o=1))
+                nc.sync.dma_start(out=lim_rows[0:NB, :], in_=limit.rearrange("(b p) -> b p", p=P))
+            elif k == 1:
+                nc.sync.dma_start(out=words[:], in_=proj_words.rearrange("g p n -> p g n"))
+            elif k == 2:
+                for q in range(4):
+                    nc.sync.dma_start(out=planes[32 * q : 32 * q + 4, :, :].bitcast(I32), in_=proj_scales[:, 4 * q : 4 * q + 4, :].rearrange("g q n -> q g n").bitcast(I32))
+            else:
+                s = k - 3
+                nc.sync.dma_start(out=mt[:, 4 * s : 4 * s + 4, :], in_=m_view[:, 4 * s : 4 * s + 4, :])
+                nc.sync.dma_start(out=vt[:, 4 * s : 4 * s + 4, :], in_=v_view[:, 4 * s : 4 * s + 4, :])
+
+        steps = {"load_x": load_x, "load_gate": load_gate, "load_dh": load_dh, "load_acc": load_acc, "late": late, "silu": silu, "dmul": dmul, "dq": dq, "widen": widen, "inter": inter, "xq": xq, "amm": amm, "add": add, "sqr": sqr, "vectors": vectors, "ars": ars, "clip": clip, "cmul": cmul, "tr": tr, "cpt": cpt, "cq": cq, "lmm": lmm, "esq": esq, "em": em, "ev9": ev9, "ev": ev, "emn": emn, "ers": ers, "est": est}
+        for s in SEQ:
+            steps[s[0]](*s[1:])

@@ -26,15 +26,18 @@ VECTOR_WIDEN = ((0, 0),)
 SCALAR_INTER = ((0, 3),(1, 3))
 G_DMUL = ((0, 2), (1, 2), (0, 3), (1, 3))
 G_EPI = 7
-SEQ = (("load_x", 0, 0,), ("widen", 0, 0,), ("load_gate", 0, 0,), ("inter", 0, 0,), ("load_x", 1, 0,), ("load_dh", 0, 0,), ("load_gate", 1, 0,), ("silu", 0, 0,), ("widen", 1, 0,), ("xq", 0, 0,), ("dmul", 0, 0,), ("inter", 1, 0,), ("silu", 1, 0,), ("load_dh", 1, 0,), ("silu", 0, 1,), ("dq", 0, 0,), ("load_acc", 0,), ("dmul", 1, 0,), ("dmul", 0, 1,), ("dq", 0, 1,), ("dq", 1, 0,), ("xq", 1, 0,), ("amm", 0, 0,), ("widen", 0, 1,), ("inter", 0, 1,), ("silu", 1, 1,), ("dmul", 1, 1,), ("widen", 1, 1,), ("xq", 0, 1,), ("load_gate", 1, 1,), ("inter", 1, 1,), ("load_x", 0, 1,), ("widen", 0, 2,), ("inter", 0, 2,), ("load_dh", 0, 1,), ("xq", 1, 1,), ("amm", 0, 1,), ("load_gate", 0, 1,), ("silu", 0, 2,), ("load_acc", 7,), ("load_x", 1, 1,), ("add", 0, 0,), ("add", 0, 1,), ("dmul", 0, 2,), ("silu", 1, 2,), ("widen", 1, 2,), ("inter", 1, 2,), ("dq", 1, 1,), ("load_acc", 3,), ("widen", 1, 3,), ("load_acc", 1,), ("xq", 0, 2,), ("xq", 1, 2,), ("load_dh", 1, 1,), ("widen", 0, 3,), ("amm", 1, 0,), ("amm", 1, 1,), ("add", 1, 0,), ("inter", 1, 3,), ("amm", 0, 2,), ("inter", 0, 3,), ("load_acc", 2,), ("add", 1, 1,), ("load_acc", 4,), ("amm", 2, 0,), ("add", 0, 2,), ("late", 1,), ("add", 2, 0,), ("late", 3,), ("dmul", 1, 2,), ("dq", 0, 2,), ("amm", 2, 1,), ("amm", 1, 2,), ("xq", 1, 3,), ("xq", 0, 3,), ("amm", 0, 3,), ("add", 2, 1,), ("add", 0, 3,), ("late", 0,), ("amm", 2, 3,), ("vectors",), ("dq", 1, 2,), ("silu", 1, 3,), ("silu", 0, 3,), ("late", 4,), ("add", 1, 2,), ("add", 2, 3,), ("sqr", 0,), ("amm", 1, 3,), ("ars", 0,), ("late", 2,), ("amm", 2, 2,), ("add", 1, 3,), ("sqr", 1,), ("add", 2, 2,), ("amm", 3, 0,), ("dmul", 1, 3,), ("ars", 1,), ("dq", 1, 3,), ("clip", 0,), ("cmul", 0, 0,), ("cmul", 0, 1,), ("amm", 3, 2,), ("clip", 1,), ("tr", 0, 0,), ("add", 3, 0,), ("cpt", 0, 0,), ("tr", 0, 1,), ("cmul", 1, 0,), ("cpt", 0, 1,), ("load_acc", 6,), ("amm", 3, 1,), ("load_acc", 5,), ("cq", 0,), ("add", 3, 2,), ("dmul", 0, 3,), ("ev9", 0,), ("tr", 1, 0,), ("lmm", 0,), ("amm", 3, 3,), ("sqr", 2,), ("ars", 2,), ("cmul", 1, 1,), ("add", 3, 1,), ("tr", 1, 1,), ("em", 0,), ("cpt", 1, 0,), ("cpt", 1, 1,), ("amm", 4, 0,), ("amm", 5, 0,), ("clip", 2,), ("esq", 0,), ("emn", 0,), ("ev9", 7,), ("ev", 0,), ("add", 3, 3,), ("cmul", 2, 0,), ("sqr", 3,), ("ars", 3,), ("amm", 4, 1,), ("add", 4, 0,), ("add", 5, 0,), ("add", 4, 1,), ("cq", 1,), ("tr", 2, 0,), ("amm", 4, 2,), ("add", 4, 2,), ("cmul", 2, 1,), ("clip", 3,), ("amm", 5, 1,), ("add", 5, 1,), ("lmm", 1,), ("ev9", 1,), ("amm", 4, 3,), ("tr", 2, 1,), ("add", 4, 3,), ("cpt", 2, 0,), ("amm", 5, 2,), ("ers", 0,), ("esq", 1,), ("cpt", 2, 1,), ("amm", 5, 3,), ("est", 0,), ("em", 1,), ("cmul", 3, 0,), ("tr", 3, 0,), ("ev", 1,), ("cq", 2,), ("add", 5, 2,), ("sqr", 4,), ("lmm", 2,), ("ev9", 2,), ("dq", 0, 3,), ("cmul", 3, 1,), ("add", 5, 3,), ("emn", 1,), ("amm", 6, 0,), ("amm", 6, 1,), ("ers", 1,), ("add", 6, 0,), ("ars", 4,), ("clip", 4,), ("add", 6, 1,), ("cmul", 4, 0,), ("esq", 2,), ("cpt", 3, 0,), ("amm", 6, 3,), ("ev", 2,), ("sqr", 5,), ("tr", 3, 1,), ("amm", 6, 2,), ("cpt", 3, 1,), ("amm", 7, 0,), ("ers", 2,), ("add", 6, 3,), ("add", 6, 2,), ("ars", 5,), ("tr", 4, 0,), ("cq", 3,), ("sqr", 6,), ("amm", 7, 3,), ("em", 2,), ("clip", 5,), ("amm", 7, 1,), ("lmm", 3,), ("esq", 3,), ("add", 7, 0,), ("est", 1,), ("cmul", 4, 1,), ("amm", 7, 2,), ("tr", 4, 1,), ("em", 3,), ("add", 7, 1,), ("add", 7, 2,), ("ev9", 3,), ("ars", 6,), ("cpt", 4, 0,), ("cpt", 4, 1,), ("emn", 2,), ("est", 2,), ("add", 7, 3,), ("ev", 3,), ("cq", 4,), ("cmul", 5, 0,), ("ev9", 4,), ("clip", 6,), ("ers", 3,), ("est", 3,), ("sqr", 7,), ("lmm", 4,), ("cmul", 5, 1,), ("esq", 4,), ("emn", 3,), ("tr", 5, 0,), ("ars", 7,), ("tr", 5, 1,), ("cmul", 6, 0,), ("cpt", 5, 0,), ("ev", 4,), ("cpt", 5, 1,), ("em", 4,), ("cq", 5,), ("ers", 4,), ("est", 4,), ("tr", 6, 0,), ("clip", 7,), ("lmm", 5,), ("esq", 5,), ("cpt", 6, 0,), ("ev9", 5,), ("cmul", 6, 1,), ("em", 5,), ("tr", 6, 1,), ("cmul", 7, 0,), ("tr", 7, 0,), ("cpt", 6, 1,), ("cpt", 7, 0,), ("ev", 5,), ("cq", 6,), ("emn", 5,), ("cmul", 7, 1,), ("lmm", 6,), ("ers", 5,), ("tr", 7, 1,), ("emn", 4,), ("em", 6,), ("cpt", 7, 1,), ("ev9", 6,), ("est", 5,), ("esq", 6,), ("cq", 7,), ("lmm", 7,), ("esq", 7,), ("ev", 6,), ("ers", 6,), ("em", 7,), ("emn", 6,), ("ev", 7,), ("emn", 7,), ("ers", 7,), ("est", 6,), ("est", 7,))
-GRADS = 5
+SEQ = (("load_x", 0, 0,), ("ev9", 0, 0,), ("ev9", 1, 0,), ("ev9", 2, 0,), ("load_gate", 1, 0,), ("load_gate", 0, 0,), ("ev9", 3, 0,), ("widen", 0, 0,), ("inter", 0, 0,), ("widen", 0, 1,), ("silu", 1, 0,), ("load_x", 1, 0,), ("late", 0,), ("silu", 0, 0,), ("inter", 0, 1,), ("xq", 0, 0,), ("vectors",), ("load_dh", 1, 0,), ("load_dh", 0, 0,), ("xq", 0, 1,), ("ev9", 4, 0,), ("widen", 1, 0,), ("load_x", 0, 1,), ("dmul", 1, 0,), ("inter", 1, 0,), ("dmul", 0, 0,), ("widen", 1, 1,), ("widen", 0, 2,), ("load_acc", 6,), ("load_acc", 3,), ("inter", 1, 1,), ("xq", 1, 0,), ("load_x", 1, 1,), ("inter", 0, 2,), ("load_gate", 0, 1,), ("load_acc", 0,), ("silu", 1, 1,), ("xq", 1, 1,), ("late", 1,), ("silu", 0, 1,), ("xq", 0, 2,), ("load_acc", 2,), ("dq", 1, 0,), ("widen", 1, 2,), ("load_acc", 7,), ("dq", 0, 0,), ("ev9", 5, 0,), ("dmul", 1, 1,), ("inter", 1, 2,), ("dmul", 0, 1,), ("xq", 1, 2,), ("widen", 0, 3,), ("inter", 0, 3,), ("load_dh", 1, 1,), ("amm", 0, 0,), ("add", 0, 0,), ("xq", 0, 3,), ("dq", 1, 1,), ("dq", 0, 1,), ("ev9", 6, 0,), ("amm", 0, 1,), ("amm", 1, 0,), ("load_acc", 1,), ("widen", 1, 3,), ("add", 0, 1,), ("add", 1, 0,), ("inter", 1, 3,), ("amm", 1, 1,), ("amm", 0, 2,), ("add", 1, 1,), ("xq", 1, 3,), ("load_gate", 1, 1,), ("add", 0, 2,), ("silu", 1, 2,), ("amm", 1, 2,), ("silu", 0, 2,), ("add", 1, 2,), ("amm", 0, 3,), ("amm", 2, 0,), ("late", 4,), ("amm", 1, 3,), ("load_dh", 0, 1,), ("add", 0, 3,), ("add", 2, 0,), ("add", 1, 3,), ("dmul", 1, 2,), ("dmul", 0, 2,), ("amm", 3, 0,), ("amm", 2, 1,), ("late", 3,), ("add", 3, 0,), ("amm", 3, 1,), ("add", 2, 1,), ("load_acc", 5,), ("add", 3, 1,), ("amm", 3, 2,), ("silu", 1, 3,), ("sqr", 0,), ("amm", 2, 2,), ("silu", 0, 3,), ("add", 3, 2,), ("ars", 0,), ("sqr", 1,), ("amm", 3, 3,), ("clip", 0,), ("add", 2, 2,), ("add", 3, 3,), ("dq", 1, 2,), ("amm", 2, 3,), ("dq", 0, 2,), ("ars", 1,), ("dmul", 1, 3,), ("clip", 1,), ("add", 2, 3,), ("dmul", 0, 3,), ("cmul", 0, 0,), ("cmul", 0, 1,), ("ev9", 7, 0,), ("amm", 4, 0,), ("amm", 4, 1,), ("load_acc", 4,), ("sqr", 3,), ("amm", 4, 2,), ("add", 4, 0,), ("amm", 4, 3,), ("add", 4, 1,), ("add", 4, 2,), ("cmul", 1, 0,), ("cmul", 1, 1,), ("add", 4, 3,), ("tr", 0, 0,), ("tr", 0, 1,), ("sqr", 2,), ("amm", 5, 0,), ("cpt", 0, 0,), ("ars", 2,), ("dq", 1, 3,), ("amm", 5, 1,), ("late", 2,), ("cpt", 0, 1,), ("clip", 2,), ("add", 5, 0,), ("amm", 5, 2,), ("dq", 0, 3,), ("add", 5, 1,), ("amm", 5, 3,), ("tr", 1, 0,), ("add", 5, 2,), ("tr", 1, 1,), ("add", 5, 3,), ("cpt", 1, 0,), ("cq", 0, 0,), ("cpt", 1, 1,), ("ars", 3,), ("sqr", 4,), ("clip", 3,), ("amm", 6, 0,), ("cmul", 2, 0,), ("cmul", 2, 1,), ("cq", 1, 0,), ("add", 6, 0,), ("lmm", 0, 0,), ("esq", 0, 0,), ("sqr", 5,), ("em", 0, 0,), ("tr", 2, 0,), ("tr", 2, 1,), ("cmul", 3, 0,), ("cmul", 3, 1,), ("ev", 0, 0,), ("ars", 4,), ("cpt", 2, 0,), ("clip", 4,), ("cpt", 2, 1,), ("amm", 6, 1,), ("lmm", 1, 0,), ("emn", 0, 0,), ("esq", 1, 0,), ("em", 1, 0,), ("add", 6, 1,), ("tr", 3, 0,), ("tr", 3, 1,), ("ev", 1, 0,), ("cq", 2, 0,), ("cpt", 3, 0,), ("ers", 0, 0,), ("cpt", 3, 1,), ("emn", 1, 0,), ("ars", 5,), ("cmul", 4, 0,), ("cmul", 4, 1,), ("clip", 5,), ("amm", 6, 2,), ("add", 6, 2,), ("cq", 3, 0,), ("ers", 1, 0,), ("lmm", 2, 0,), ("est", 0, 0,), ("esq", 2, 0,), ("tr", 4, 0,), ("em", 2, 0,), ("tr", 4, 1,), ("amm", 7, 0,), ("cpt", 4, 0,), ("ev", 2, 0,), ("cpt", 4, 1,), ("add", 7, 0,), ("cmul", 5, 0,), ("cmul", 5, 1,), ("est", 1, 0,), ("amm", 6, 3,), ("emn", 2, 0,), ("lmm", 3, 0,), ("amm", 7, 1,), ("add", 6, 3,), ("cq", 4, 0,), ("add", 7, 1,), ("tr", 5, 0,), ("tr", 5, 1,), ("ers", 2, 0,), ("amm", 7, 2,), ("esq", 3, 0,), ("cpt", 5, 0,), ("em", 3, 0,), ("cpt", 5, 1,), ("add", 7, 2,), ("ev", 3, 0,), ("amm", 7, 3,), ("lmm", 4, 0,), ("est", 2, 0,), ("cq", 5, 0,), ("emn", 3, 0,), ("sqr", 6,), ("add", 7, 3,), ("ars", 6,), ("clip", 6,), ("ers", 3, 0,), ("esq", 4, 0,), ("em", 4, 0,), ("lmm", 5, 0,), ("ev", 4, 0,), ("cmul", 6, 0,), ("cmul", 6, 1,), ("sqr", 7,), ("est", 3, 0,), ("ars", 7,), ("clip", 7,), ("emn", 4, 0,), ("tr", 6, 0,), ("tr", 6, 1,), ("ers", 4, 0,), ("cpt", 6, 0,), ("cpt", 6, 1,), ("cmul", 7, 0,), ("cmul", 7, 1,), ("esq", 5, 0,), ("em", 5, 0,), ("cq", 6, 0,), ("est", 4, 0,), ("ev", 5, 0,), ("tr", 7, 0,), ("tr", 7, 1,), ("emn", 5, 0,), ("cpt", 7, 0,), ("cpt", 7, 1,), ("lmm", 6, 0,), ("ers", 5, 0,), ("cq", 7, 0,), ("cq", 7, 1,), ("esq", 6, 0,), ("em", 6, 0,), ("est", 5, 0,), ("ev", 6, 0,), ("emn", 6, 0,), ("lmm", 7, 0,), ("lmm", 7, 1,), ("ers", 6, 0,), ("est", 6, 0,), ("esq", 7, 0,), ("esq", 7, 1,), ("em", 7, 0,), ("em", 7, 1,), ("ev", 7, 0,), ("ev", 7, 1,), ("emn", 7, 0,), ("emn", 7, 1,), ("ers", 7, 0,), ("ers", 7, 1,), ("est", 7, 0,), ("est", 7, 1,))
+PARTS = (1, 1, 1, 1, 1, 1, 1, 2)
+DW = 256
+HALVES = (1, 1, 1, 1, 1, 1, 1, 2)
+GRADS = 4
 
 
 def tile_galore_up_projection_f1_kernel(tc, x_bytes, x_scale, dh, gate, acc, limit, precond, proj_words, proj_scales, m, v, out_0, out_1, out_2):
     nc = tc.nc
     with ExitStack() as ctx:
         keep = ctx.enter_context(tc.tile_pool(name="keep", bufs=1))
-        stream = ctx.enter_context(tc.tile_pool(name="stream", bufs=10))
+        stream = ctx.enter_context(tc.tile_pool(name="stream", bufs=12))
         work = ctx.enter_context(tc.tile_pool(name="work", bufs=2))
         ps_p = ctx.enter_context(tc.psum_pool(name="ps_p", bufs=1))
         ps_a = ctx.enter_context(tc.psum_pool(name="ps_a", bufs=3))
@@ -47,7 +50,7 @@ def tile_galore_up_projection_f1_kernel(tc, x_bytes, x_scale, dh, gate, acc, lim
         nc.scalar.activation(out=warm[:], in_=warm[:], func=ACT.Silu)
         xs = keep.tile([P, NG1, 4], F32, name="xs")
         nc.sync.dma_start(out=xs[:], in_=x_scale.rearrange("(g p t) o -> p g (t o)", p=P, t=4))
-        pc_rows = keep.tile([P, I], BF16, name="pc_rows")
+        pc_rows = work.tile([P, I], BF16, name="pc_rows", tag="t_c")
         nc.gpsimd.memset(pc_rows[:].bitcast(I32), 0)
         ones = keep.tile([P, P], BF16, name="ones")
         nc.gpsimd.memset(ones[:], 1.0)
@@ -113,20 +116,25 @@ def tile_galore_up_projection_f1_kernel(tc, x_bytes, x_scale, dh, gate, acc, lim
         ep = {}
 
         def silu(g, q):
-            cols = slice(256 * (q % 2), 256 * (q % 2) + 256)
-            t_s = work.tile([P, 4, 256], F32, name="t_s", bufs=2)
-            nc.scalar.activation(out=t_s[:], in_=gt[g, q // 2][:, :, cols], func=ACT.Silu)
+            lo = DW * q % 512
+            t_s = work.tile([P, 4, DW], F32, name="t_s", bufs=3)
+            nc.scalar.activation(out=t_s[:], in_=gt[g, DW * q // 512][:, :, lo : lo + DW], func=ACT.Silu)
             ts_[g, q] = t_s
 
         def dmul(g, q):
-            cols = slice(256 * (q % 2), 256 * (q % 2) + 256)
-            t_di = work.tile([P, 256, 4], BF16, name="t_di", align_bytes=64)
+            lo = DW * q % 512
+            t_di = work.tile([P, DW, 4], BF16, name="t_di", align_bytes=64)
             eng = nc.gpsimd if (g, q) in G_DMUL else nc.vector
-            eng.tensor_tensor(out=t_di[:], in0=ts_[g, q][:].rearrange("p t n -> p n t"), in1=dt[g, q // 2][:, :, cols].rearrange("p t n -> p n t"), op=ALU.mult)
+            eng.tensor_tensor(
+                out=t_di[:].rearrange("p (c i) t -> p c t i", i=8),
+                in0=ts_[g, q][:].rearrange("p t (c i) -> p c t i", i=8),
+                in1=dt[g, DW * q // 512][:, :, lo : lo + DW].rearrange("p t (c i) -> p c t i", i=8),
+                op=ALU.mult,
+            )
             tdi[g, q] = t_di
 
         def dq(g, q):
-            o_cols = slice(256 * q, 256 * q + 256)
+            o_cols = slice(DW * q, DW * q + DW)
             nc.vector.quantize_mx(out=d_codes[:, g, o_cols].bitcast(FP8X4), scales=d_scales[:, g, o_cols], in_=tdi[g, q][:].rearrange("p n t -> p (n t)"))
 
         def widen(g, j):
@@ -145,7 +153,7 @@ def tile_galore_up_projection_f1_kernel(tc, x_bytes, x_scale, dh, gate, acc, lim
             if (g, j) in SCALAR_INTER:
                 nc.scalar.copy(out=t_xi[:], in_=tw[g, j][:].rearrange("p t n -> p n t"))
             else:
-                nc.vector.tensor_copy(out=t_xi[:], in_=tw[g, j][:].rearrange("p t n -> p n t"))
+                nc.vector.tensor_copy(out=t_xi[:].rearrange("p (c i) t -> p c t i", i=4), in_=tw[g, j][:].rearrange("p t (c i) -> p c t i", i=4))
             txi[g, j] = t_xi
 
         def xq(g, j):
@@ -192,18 +200,18 @@ def tile_galore_up_projection_f1_kernel(tc, x_bytes, x_scale, dh, gate, acc, lim
                 nc.tensor.matmul(pc[:, cols], lhsT=ones[:], rhs=pc_rows[:, cols], start=True, stop=True)
 
         def ars(b):
-            t_r = work.tile([P, 1], F32, name="t_r")
+            t_r = work.tile([P, 1], F32, name="t_r", bufs=2)
             nc.scalar.activation(out=t_r[:], in_=ss[b][:], func=ACT.Abs_reciprocal_sqrt, scale=1.0 / I)
             rr[b] = t_r
 
         def clip(b):
-            t_clip = work.tile([P, 1], F32, name="t_clip")
-            nc.vector.tensor_scalar(out=t_clip[:], in0=rr[b][:], scalar1=lim[:, b : b + 1], scalar2=1.0, op0=ALU.mult, op1=ALU.min)
+            t_clip = work.tile([P, 1], F32, name="t_clip", bufs=2)
+            nc.gpsimd.tensor_scalar(out=t_clip[:], in0=rr[b][:], scalar1=lim[:, b : b + 1], scalar2=1.0, op0=ALU.mult, op1=ALU.min)
             cl[b] = t_clip
 
         def cmul(b, h):
             if h == 0:
-                t_c = work.tile([P, I], BF16, name="t_c")
+                t_c = work.tile([P, I], BF16, name="t_c", tag="t_c")
                 tcb[b] = t_c
             cols = slice(1024 * h, 1024 * h + 1024)
             nc.vector.scalar_tensor_tensor(out=tcb[b][:, cols], in0=grad[b][:, cols], scalar=cl[b][:], in1=pc[:, cols], op0=ALU.mult, op1=ALU.mult)
@@ -223,16 +231,24 @@ def tile_galore_up_projection_f1_kernel(tc, x_bytes, x_scale, dh, gate, acc, lim
                 tct[b] = t_ct
             nc.scalar.copy(out=tct[b][:, 2 * h : 2 * h + 2, :, :].rearrange("p g o t -> p g (o t)").bitcast(F32).rearrange("p g (o u) -> p g o u", u=2), in_=ctp[b, h][:].rearrange("p k u o -> p k o u"))
 
-        def cq(b):
-            t_cq = work.tile([P, NG2 * P], U32, name="t_cq", align_bytes=64)
-            t_cs = work.tile([P, NG2 * P], U8, name="t_cs", align_bytes=64)
-            nc.vector.quantize_mx(out=t_cq[:].bitcast(FP8X4), scales=t_cs[:], in_=tct[b][:].rearrange("p g o t -> p (g o t)"))
-            cqs[b] = (t_cq, t_cs)
-
-        def lmm(b):
+        def cq(b, h):
+            if h == 0:
+                t_cq = work.tile([P, NG2 * P], U32, name="t_cq", align_bytes=64)
+                t_cs = work.tile([P, NG2 * P], U8, name="t_cs", align_bytes=64)
+                cqs[b] = (t_cq, t_cs)
             t_cq, t_cs = cqs[b]
-            low = ps_l.tile([P, R], F32, name="low")
-            for g in range(NG2):
+            width = NG2 // HALVES[b]
+            cols = slice(P * width * h, P * width * h + P * width)
+            nc.vector.quantize_mx(out=t_cq[:, cols].bitcast(FP8X4), scales=t_cs[:, cols], in_=tct[b][:, width * h : width * h + width, :, :].rearrange("p g o t -> p (g o t)"))
+
+        def lmm(b, h):
+            t_cq, t_cs = cqs[b]
+            if h == 0:
+                low = ps_l.tile([P, R], F32, name="low")
+                lows[b] = low
+            low = lows[b]
+            width = NG2 // HALVES[b]
+            for g in range(width * h, width * h + width):
                 nc.tensor.matmul_mx(
                     out=low[:],
                     lhsT=t_cq[:, P * g : P * g + P].bitcast(FP8X4),
@@ -242,54 +258,71 @@ def tile_galore_up_projection_f1_kernel(tc, x_bytes, x_scale, dh, gate, acc, lim
                     start=(g == 0),
                     stop=(g == NG2 - 1),
                 )
-            lows[b] = low
 
         def on_g(b):
             return b < G_EPI
 
-        def esq(b):
-            t_sq = work.tile([P, R], F32, name="t_sq")
-            nc.scalar.activation(out=t_sq[:], in_=lows[b][:], func=ACT.Square, scale=sqrt(0.1))
-            ep[b, "sq"] = t_sq
+        def part(b, c):
+            width = R // PARTS[b]
+            return slice(width * c, width * c + width)
 
-        def em(b):
-            t_m = work.tile([P, R], F32, name="t_m")
-            nc.vector.scalar_tensor_tensor(out=t_m[:], in0=lows[b][:], scalar=0.25, in1=mt[:, b, :], op0=ALU.mult, op1=ALU.add)
-            ep[b, "m"] = t_m
+        def esq(b, c):
+            if c == 0:
+                t_sq = work.tile([P, R], F32, name="t_sq", bufs=1)
+                ep[b, "sq"] = t_sq
+            k = part(b, c)
+            nc.scalar.activation(out=ep[b, "sq"][:, k], in_=lows[b][:, k], func=ACT.Square, scale=sqrt(0.1))
 
-        def ev9(b):
-            if on_g(b):
+        def em(b, c):
+            if c == 0:
+                t_m = work.tile([P, R], F32, name="t_m", bufs=2)
+                ep[b, "m"] = t_m
+            k = part(b, c)
+            nc.vector.scalar_tensor_tensor(out=ep[b, "m"][:, k], in0=lows[b][:, k], scalar=0.25, in1=mt[:, b, k], op0=ALU.mult, op1=ALU.add)
+
+        def ev9(b, c):
+            if b < 0:
                 t_v9 = work.tile([P, R], F32, name="t_v9", bufs=1)
                 nc.gpsimd.tensor_scalar(out=t_v9[:], in0=vt[:, b, :], scalar1=0.9, scalar2=0.0, op0=ALU.mult, op1=ALU.add)
                 ep[b, "v9"] = t_v9
 
-        def ev(b):
-            t_v = work.tile([P, R], F32, name="t_v", bufs=3)
-            if on_g(b):
-                nc.gpsimd.tensor_tensor(out=t_v[:], in0=ep[b, "v9"][:], in1=ep[b, "sq"][:], op=ALU.add)
+        def ev(b, c):
+            if c == 0:
+                t_v = work.tile([P, R], F32, name="t_v", bufs=2)
+                ep[b, "v"] = t_v
+            k = part(b, c)
+            t_v = ep[b, "v"]
+            if b < 0:
+                nc.gpsimd.tensor_tensor(out=t_v[:, k], in0=ep[b, "v9"][:, k], in1=ep[b, "sq"][:, k], op=ALU.add)
             else:
-                nc.vector.scalar_tensor_tensor(out=t_v[:], in0=vt[:, b, :], scalar=0.9, in1=ep[b, "sq"][:], op0=ALU.mult, op1=ALU.add)
-            nc.sync.dma_start(out=out_1[P * b : P * b + P, :], in_=t_v[:])
-            ep[b, "v"] = t_v
+                nc.vector.scalar_tensor_tensor(out=t_v[:, k], in0=vt[:, b, k], scalar=0.9, in1=ep[b, "sq"][:, k], op0=ALU.mult, op1=ALU.add)
+            nc.sync.dma_start(out=out_1[P * b : P * b + P, k], in_=t_v[:, k])
 
-        def emn(b):
-            t_mn = work.tile([P, R], F32, name="t_mn", bufs=3)
+        def emn(b, c):
+            if c == 0:
+                t_mn = work.tile([P, R], F32, name="t_mn", bufs=2)
+                ep[b, "mn"] = t_mn
+            k = part(b, c)
+            t_mn = ep[b, "mn"]
             if on_g(b):
-                nc.gpsimd.tensor_scalar(out=t_mn[:], in0=ep[b, "m"][:], scalar1=0.8, scalar2=0.0, op0=ALU.mult, op1=ALU.add)
+                nc.gpsimd.tensor_scalar(out=t_mn[:, k], in0=ep[b, "m"][:, k], scalar1=0.8, scalar2=0.0, op0=ALU.mult, op1=ALU.add)
             else:
-                nc.scalar.activation(out=t_mn[:], in_=ep[b, "m"][:], func=ACT.Copy, scale=0.8)
-            nc.sync.dma_start(out=out_0[P * b : P * b + P, :], in_=t_mn[:])
+                nc.scalar.activation(out=t_mn[:, k], in_=ep[b, "m"][:, k], func=ACT.Copy, scale=0.8)
+            nc.sync.dma_start(out=out_0[P * b : P * b + P, k], in_=t_mn[:, k])
 
-        def ers(b):
-            t_rs = work.tile([P, R], F32, name="t_rs", bufs=3)
-            nc.scalar.activation(out=t_rs[:], in_=ep[b, "v"][:], func=ACT.Abs_reciprocal_sqrt, scale=1.0 / 0.64)
-            ep[b, "rs"] = t_rs
+        def ers(b, c):
+            if c == 0:
+                t_rs = work.tile([P, R], F32, name="t_rs", bufs=2)
+                ep[b, "rs"] = t_rs
+            k = part(b, c)
+            nc.scalar.activation(out=ep[b, "rs"][:, k], in_=ep[b, "v"][:, k], func=ACT.Abs_reciprocal_sqrt, scale=1.0 / 0.64)
 
-        def est(b):
+        def est(b, c):
+            k = part(b, c)
             t_st = ep[b, "rs"]
             eng = nc.gpsimd if on_g(b) else nc.vector
-            eng.tensor_tensor(out=t_st[:], in0=ep[b, "m"][:], in1=ep[b, "rs"][:], op=ALU.mult)
-            nc.sync.dma_start(out=out_2[P * b : P * b + P, :], in_=t_st[:])
+            eng.tensor_tensor(out=t_st[:, k], in0=ep[b, "m"][:, k], in1=t_st[:, k], op=ALU.mult)
+            nc.sync.dma_start(out=out_2[P * b : P * b + P, k], in_=t_st[:, k])
 
         def late(k):
             if k == 0:

from contextlib import ExitStack
from math import sqrt

import concourse.mybir as mybir
from concourse.masks import make_identity

T, O, I, R = 1024, 1024, 2048, 512
FLOPS = 2 * T * O * I + 2 * O * I * R

F32 = mybir.dt.float32
BF16 = mybir.dt.bfloat16
I32 = mybir.dt.int32
U32 = mybir.dt.uint32
U8 = mybir.dt.uint8
E4M3FN = mybir.dt.float8_e4m3fn
FP8X4 = mybir.dt.float8_e4m3fn_x4
FP4X4 = mybir.dt.float4_e2m1fn_x4
ACT = mybir.ActivationFunctionType
ALU = mybir.AluOpType

P = 128
NB = O // P
NG1 = T // 512
NG2 = I // 512
VECTOR_WIDEN = ((0, 0),)
SCALAR_INTER = ((0, 3),(1, 3))
G_DMUL = ((0, 2), (1, 2), (0, 3), (1, 3))
G_EPI = 7
SEQ = (("load_x", 0, 0,), ("ev9", 0, 0,), ("ev9", 1, 0,), ("ev9", 2, 0,), ("load_gate", 1, 0,), ("load_gate", 0, 0,), ("ev9", 3, 0,), ("widen", 0, 0,), ("inter", 0, 0,), ("widen", 0, 1,), ("silu", 1, 0,), ("load_x", 1, 0,), ("late", 0,), ("silu", 0, 0,), ("inter", 0, 1,), ("xq", 0, 0,), ("vectors",), ("load_dh", 1, 0,), ("load_dh", 0, 0,), ("xq", 0, 1,), ("ev9", 4, 0,), ("widen", 1, 0,), ("load_x", 0, 1,), ("dmul", 1, 0,), ("inter", 1, 0,), ("dmul", 0, 0,), ("widen", 1, 1,), ("widen", 0, 2,), ("load_acc", 6,), ("load_acc", 3,), ("inter", 1, 1,), ("xq", 1, 0,), ("load_x", 1, 1,), ("inter", 0, 2,), ("load_gate", 0, 1,), ("load_acc", 0,), ("silu", 1, 1,), ("xq", 1, 1,), ("late", 1,), ("silu", 0, 1,), ("xq", 0, 2,), ("load_acc", 2,), ("dq", 1, 0,), ("widen", 1, 2,), ("load_acc", 7,), ("dq", 0, 0,), ("ev9", 5, 0,), ("dmul", 1, 1,), ("inter", 1, 2,), ("dmul", 0, 1,), ("xq", 1, 2,), ("widen", 0, 3,), ("inter", 0, 3,), ("load_dh", 1, 1,), ("amm", 0, 0,), ("add", 0, 0,), ("xq", 0, 3,), ("dq", 1, 1,), ("dq", 0, 1,), ("ev9", 6, 0,), ("amm", 0, 1,), ("amm", 1, 0,), ("load_acc", 1,), ("widen", 1, 3,), ("add", 0, 1,), ("add", 1, 0,), ("inter", 1, 3,), ("amm", 1, 1,), ("amm", 0, 2,), ("add", 1, 1,), ("xq", 1, 3,), ("load_gate", 1, 1,), ("add", 0, 2,), ("silu", 1, 2,), ("amm", 1, 2,), ("silu", 0, 2,), ("add", 1, 2,), ("amm", 0, 3,), ("amm", 2, 0,), ("late", 4,), ("amm", 1, 3,), ("load_dh", 0, 1,), ("add", 0, 3,), ("add", 2, 0,), ("add", 1, 3,), ("dmul", 1, 2,), ("dmul", 0, 2,), ("amm", 3, 0,), ("amm", 2, 1,), ("late", 3,), ("add", 3, 0,), ("amm", 3, 1,), ("add", 2, 1,), ("load_acc", 5,), ("add", 3, 1,), ("amm", 3, 2,), ("silu", 1, 3,), ("sqr", 0,), ("amm", 2, 2,), ("silu", 0, 3,), ("add", 3, 2,), ("ars", 0,), ("sqr", 1,), ("amm", 3, 3,), ("clip", 0,), ("add", 2, 2,), ("add", 3, 3,), ("dq", 1, 2,), ("amm", 2, 3,), ("dq", 0, 2,), ("ars", 1,), ("dmul", 1, 3,), ("clip", 1,), ("add", 2, 3,), ("dmul", 0, 3,), ("cmul", 0, 0,), ("cmul", 0, 1,), ("ev9", 7, 0,), ("amm", 4, 0,), ("amm", 4, 1,), ("load_acc", 4,), ("sqr", 3,), ("amm", 4, 2,), ("add", 4, 0,), ("amm", 4, 3,), ("add", 4, 1,), ("add", 4, 2,), ("cmul", 1, 0,), ("cmul", 1, 1,), ("add", 4, 3,), ("tr", 0, 0,), ("tr", 0, 1,), ("sqr", 2,), ("amm", 5, 0,), ("cpt", 0, 0,), ("ars", 2,), ("dq", 1, 3,), ("amm", 5, 1,), ("late", 2,), ("cpt", 0, 1,), ("clip", 2,), ("add", 5, 0,), ("amm", 5, 2,), ("dq", 0, 3,), ("add", 5, 1,), ("amm", 5, 3,), ("tr", 1, 0,), ("add", 5, 2,), ("tr", 1, 1,), ("add", 5, 3,), ("cpt", 1, 0,), ("cq", 0, 0,), ("cpt", 1, 1,), ("ars", 3,), ("sqr", 4,), ("clip", 3,), ("amm", 6, 0,), ("cmul", 2, 0,), ("cmul", 2, 1,), ("cq", 1, 0,), ("add", 6, 0,), ("lmm", 0, 0,), ("esq", 0, 0,), ("sqr", 5,), ("em", 0, 0,), ("tr", 2, 0,), ("tr", 2, 1,), ("cmul", 3, 0,), ("cmul", 3, 1,), ("ev", 0, 0,), ("ars", 4,), ("cpt", 2, 0,), ("clip", 4,), ("cpt", 2, 1,), ("amm", 6, 1,), ("lmm", 1, 0,), ("emn", 0, 0,), ("esq", 1, 0,), ("em", 1, 0,), ("add", 6, 1,), ("tr", 3, 0,), ("tr", 3, 1,), ("ev", 1, 0,), ("cq", 2, 0,), ("cpt", 3, 0,), ("ers", 0, 0,), ("cpt", 3, 1,), ("emn", 1, 0,), ("ars", 5,), ("cmul", 4, 0,), ("cmul", 4, 1,), ("clip", 5,), ("amm", 6, 2,), ("add", 6, 2,), ("cq", 3, 0,), ("ers", 1, 0,), ("lmm", 2, 0,), ("est", 0, 0,), ("esq", 2, 0,), ("tr", 4, 0,), ("em", 2, 0,), ("tr", 4, 1,), ("amm", 7, 0,), ("cpt", 4, 0,), ("ev", 2, 0,), ("cpt", 4, 1,), ("add", 7, 0,), ("cmul", 5, 0,), ("cmul", 5, 1,), ("est", 1, 0,), ("amm", 6, 3,), ("emn", 2, 0,), ("lmm", 3, 0,), ("amm", 7, 1,), ("add", 6, 3,), ("cq", 4, 0,), ("add", 7, 1,), ("tr", 5, 0,), ("tr", 5, 1,), ("ers", 2, 0,), ("amm", 7, 2,), ("esq", 3, 0,), ("cpt", 5, 0,), ("em", 3, 0,), ("cpt", 5, 1,), ("add", 7, 2,), ("ev", 3, 0,), ("amm", 7, 3,), ("lmm", 4, 0,), ("est", 2, 0,), ("cq", 5, 0,), ("emn", 3, 0,), ("sqr", 6,), ("add", 7, 3,), ("ars", 6,), ("clip", 6,), ("ers", 3, 0,), ("esq", 4, 0,), ("em", 4, 0,), ("lmm", 5, 0,), ("ev", 4, 0,), ("cmul", 6, 0,), ("cmul", 6, 1,), ("sqr", 7,), ("est", 3, 0,), ("ars", 7,), ("clip", 7,), ("emn", 4, 0,), ("tr", 6, 0,), ("tr", 6, 1,), ("ers", 4, 0,), ("cpt", 6, 0,), ("cpt", 6, 1,), ("cmul", 7, 0,), ("cmul", 7, 1,), ("esq", 5, 0,), ("em", 5, 0,), ("cq", 6, 0,), ("est", 4, 0,), ("ev", 5, 0,), ("tr", 7, 0,), ("tr", 7, 1,), ("emn", 5, 0,), ("cpt", 7, 0,), ("cpt", 7, 1,), ("lmm", 6, 0,), ("ers", 5, 0,), ("cq", 7, 0,), ("cq", 7, 1,), ("esq", 6, 0,), ("em", 6, 0,), ("est", 5, 0,), ("ev", 6, 0,), ("emn", 6, 0,), ("lmm", 7, 0,), ("lmm", 7, 1,), ("ers", 6, 0,), ("est", 6, 0,), ("esq", 7, 0,), ("esq", 7, 1,), ("em", 7, 0,), ("em", 7, 1,), ("ev", 7, 0,), ("ev", 7, 1,), ("emn", 7, 0,), ("emn", 7, 1,), ("ers", 7, 0,), ("ers", 7, 1,), ("est", 7, 0,), ("est", 7, 1,))
PARTS = (1, 1, 1, 1, 1, 1, 1, 2)
DW = 256
HALVES = (1, 1, 1, 1, 1, 1, 1, 2)
GRADS = 4


def tile_galore_up_projection_f1_kernel(tc, x_bytes, x_scale, dh, gate, acc, limit, precond, proj_words, proj_scales, m, v, out_0, out_1, out_2):
    nc = tc.nc
    with ExitStack() as ctx:
        keep = ctx.enter_context(tc.tile_pool(name="keep", bufs=1))
        stream = ctx.enter_context(tc.tile_pool(name="stream", bufs=12))
        work = ctx.enter_context(tc.tile_pool(name="work", bufs=2))
        ps_p = ctx.enter_context(tc.psum_pool(name="ps_p", bufs=1))
        ps_a = ctx.enter_context(tc.psum_pool(name="ps_a", bufs=3))
        ps_t = ctx.enter_context(tc.psum_pool(name="ps_t", bufs=2))
        ps_l = ctx.enter_context(tc.psum_pool(name="ps_l", bufs=1))
        ctx.enter_context(tc.manual_schedule())

        warm = keep.tile([P, 1], F32, name="warm")
        nc.vector.memset(warm[:], 0.0)
        nc.scalar.activation(out=warm[:], in_=warm[:], func=ACT.Silu)
        xs = keep.tile([P, NG1, 4], F32, name="xs")
        nc.sync.dma_start(out=xs[:], in_=x_scale.rearrange("(g p t) o -> p g (t o)", p=P, t=4))
        pc_rows = work.tile([P, I], BF16, name="pc_rows", tag="t_c")
        nc.gpsimd.memset(pc_rows[:].bitcast(I32), 0)
        ones = keep.tile([P, P], BF16, name="ones")
        nc.gpsimd.memset(ones[:], 1.0)
        ident = keep.tile([P, P], F32, name="ident")
        make_identity(nc, ident[:])
        lim_rows = keep.tile([P, P], BF16, name="lim_rows")
        nc.gpsimd.memset(lim_rows[:], 0.0)
        planes = keep.tile([P, NG2, R], U8, name="planes", align_bytes=64)
        nc.gpsimd.memset(planes[:].rearrange("p g n -> p (g n)").bitcast(I32), 0)

        x_view = x_bytes.rearrange("(g p t) n -> g p t n", p=P, t=4)
        gate_view = gate.rearrange("(g p t) n -> g p t n", p=P, t=4)
        dh_view = dh.rearrange("(g p t) n -> g p t n", p=P, t=4)
        xb = {}
        gt = {}
        dt = {}
        at = {}

        def load_x(g, c):
            t_x = keep.tile([P, 4, 1024], U8, name="xb%d%d" % (g, c))
            nc.sync.dma_start(out=t_x[:], in_=x_view[g][:, :, 1024 * c : 1024 * c + 1024])
            xb[g, c] = t_x

        def load_gate(g, h):
            t_g = stream.tile([P, 4, 512], BF16, name="t_g", tag="stream")
            nc.sync.dma_start(out=t_g[:], in_=gate_view[g][:, :, 512 * h : 512 * h + 512])
            gt[g, h] = t_g

        def load_dh(g, h):
            t_d = stream.tile([P, 4, 512], BF16, name="t_d", tag="stream")
            nc.sync.dma_start(out=t_d[:], in_=dh_view[g][:, :, 512 * h : 512 * h + 512])
            dt[g, h] = t_d

        def load_acc(b):
            t_a = stream.tile([P, I], BF16, name="t_a", tag="stream")
            nc.sync.dma_start(out=t_a[:], in_=acc[P * b : P * b + P, :])
            at[b] = t_a

        d_codes = keep.tile([P, NG1, O], U32, name="d_codes", align_bytes=64)
        d_scales = keep.tile([P, NG1, O], U8, name="d_scales", align_bytes=64)
        x_codes = keep.tile([P, NG1, I], U32, name="x_codes", align_bytes=64)
        x_scales = keep.tile([P, NG1, I], U8, name="x_scales", align_bytes=64)
        words = keep.tile([P, NG2, 2 * R], U8, name="words", align_bytes=64)
        mt = keep.tile([P, NB, R], BF16, name="mt")
        vt = keep.tile([P, NB, R], BF16, name="vt")
        m_view = m.rearrange("(b p) r -> p b r", p=P)
        v_view = v.rearrange("(b p) r -> p b r", p=P)

        ts_ = {}
        tdi = {}
        tw = {}
        txi = {}
        aps = {}
        grad = {}
        ss = {}
        rr = {}
        cl = {}
        tcb = {}
        tct = {}
        ctp = {}
        cqs = {}
        lows = {}
        ep = {}

        def silu(g, q):
            lo = DW * q % 512
            t_s = work.tile([P, 4, DW], F32, name="t_s", bufs=3)
            nc.scalar.activation(out=t_s[:], in_=gt[g, DW * q // 512][:, :, lo : lo + DW], func=ACT.Silu)
            ts_[g, q] = t_s

        def dmul(g, q):
            lo = DW * q % 512
            t_di = work.tile([P, DW, 4], BF16, name="t_di", align_bytes=64)
            eng = nc.gpsimd if (g, q) in G_DMUL else nc.vector
            eng.tensor_tensor(
                out=t_di[:].rearrange("p (c i) t -> p c t i", i=8),
                in0=ts_[g, q][:].rearrange("p t (c i) -> p c t i", i=8),
                in1=dt[g, DW * q // 512][:, :, lo : lo + DW].rearrange("p t (c i) -> p c t i", i=8),
                op=ALU.mult,
            )
            tdi[g, q] = t_di

        def dq(g, q):
            o_cols = slice(DW * q, DW * q + DW)
            nc.vector.quantize_mx(out=d_codes[:, g, o_cols].bitcast(FP8X4), scales=d_scales[:, g, o_cols], in_=tdi[g, q][:].rearrange("p n t -> p (n t)"))

        def widen(g, j):
            c0 = 512 * (j % 2)
            t_w = work.tile([P, 4, 512], BF16, name="t_w")
            for t in range(4):
                src = xb[g, j // 2][:, t, c0 : c0 + 512].bitcast(E4M3FN)
                if (g, j) in VECTOR_WIDEN:
                    nc.vector.tensor_scalar(out=t_w[:, t, :], in0=src, scalar1=xs[:, g, t : t + 1], scalar2=None, op0=ALU.mult)
                else:
                    nc.scalar.activation(out=t_w[:, t, :], in_=src, func=ACT.Copy, scale=xs[:, g, t : t + 1])
            tw[g, j] = t_w

        def inter(g, j):
            t_xi = work.tile([P, 512, 4], BF16, name="t_xi", align_bytes=64)
            if (g, j) in SCALAR_INTER:
                nc.scalar.copy(out=t_xi[:], in_=tw[g, j][:].rearrange("p t n -> p n t"))
            else:
                nc.vector.tensor_copy(out=t_xi[:].rearrange("p (c i) t -> p c t i", i=4), in_=tw[g, j][:].rearrange("p t (c i) -> p c t i", i=4))
            txi[g, j] = t_xi

        def xq(g, j):
            i_cols = slice(512 * j, 512 * j + 512)
            nc.vector.quantize_mx(out=x_codes[:, g, i_cols].bitcast(FP8X4), scales=x_scales[:, g, i_cols], in_=txi[g, j][:].rearrange("p n t -> p (n t)"))

        def amm(b, j):
            acc_ps = ps_a.tile([P, 512], F32, name="acc_ps")
            for g in range(NG1):
                nc.tensor.matmul_mx(
                    out=acc_ps[:],
                    lhsT=d_codes[:, g, P * b : P * b + P].bitcast(FP8X4),
                    lhsT_scale=d_scales[:, g, P * b : P * b + P],
                    rhs=x_codes[:, g, 512 * j : 512 * j + 512].bitcast(FP8X4),
                    rhs_scale=x_scales[:, g, 512 * j : 512 * j + 512],
                    start=(g == 0),
                    stop=(g == NG1 - 1),
                )
            aps[b, j] = acc_ps

        def add(b, j):
            if j == 0:
                t_grad = work.tile([P, I], F32, name="t_grad", bufs=GRADS)
                grad[b] = t_grad
                t_ss = work.tile([P, 1], F32, name="t_ss", bufs=GRADS)
                ss[b] = t_ss
            nc.vector.tensor_tensor(out=grad[b][:, 512 * j : 512 * j + 512], in0=aps[b, j][:], in1=at[b][:, 512 * j : 512 * j + 512], op=ALU.add)

        def sqr(b):
            junk = work.tile([P, I], BF16, name="junk", bufs=1)
            nc.scalar.activation(out=junk[:], in_=grad[b][:], func=ACT.Square, accum_out=ss[b][:])

        lim = keep.tile([P, NB], F32, name="lim")
        lim32 = keep.tile([P, P], F32, name="lim32")
        pc = ps_p.tile([P, I], BF16, name="pc")

        def vectors():
            nc.vector.tensor_copy(out=lim32[:], in_=lim_rows[:])
            lim_ps = ps_t.tile([P, P], F32, name="lim_ps", tag="ps_t")
            nc.tensor.transpose(lim_ps[:], lim32[:], ident[:])
            nc.vector.tensor_copy(out=lim[:], in_=lim_ps[:, 0:NB])
            for c in range(4):
                cols = slice(512 * c, 512 * c + 512)
                nc.tensor.matmul(pc[:, cols], lhsT=ones[:], rhs=pc_rows[:, cols], start=True, stop=True)

        def ars(b):
            t_r = work.tile([P, 1], F32, name="t_r", bufs=2)
            nc.scalar.activation(out=t_r[:], in_=ss[b][:], func=ACT.Abs_reciprocal_sqrt, scale=1.0 / I)
            rr[b] = t_r

        def clip(b):
            t_clip = work.tile([P, 1], F32, name="t_clip", bufs=2)
            nc.gpsimd.tensor_scalar(out=t_clip[:], in0=rr[b][:], scalar1=lim[:, b : b + 1], scalar2=1.0, op0=ALU.mult, op1=ALU.min)
            cl[b] = t_clip

        def cmul(b, h):
            if h == 0:
                t_c = work.tile([P, I], BF16, name="t_c", tag="t_c")
                tcb[b] = t_c
            cols = slice(1024 * h, 1024 * h + 1024)
            nc.vector.scalar_tensor_tensor(out=tcb[b][:, cols], in0=grad[b][:, cols], scalar=cl[b][:], in1=pc[:, cols], op0=ALU.mult, op1=ALU.mult)

        def tr(b, h):
            ct_ps = ps_t.tile([P, 2, 2, P], F32, name="ct_ps", tag="ps_t")
            pairs = tcb[b][:].bitcast(F32)
            for k in range(2):
                for u in range(2):
                    base = 256 * (2 * h + k)
                    nc.tensor.transpose(ct_ps[:, k, u, :], pairs[:, base + u : base + 256 : 2], ident[:])
            ctp[b, h] = ct_ps

        def cpt(b, h):
            if h == 0:
                t_ct = work.tile([P, NG2, P, 4], BF16, name="t_ct", align_bytes=64)
                tct[b] = t_ct
            nc.scalar.copy(out=tct[b][:, 2 * h : 2 * h + 2, :, :].rearrange("p g o t -> p g (o t)").bitcast(F32).rearrange("p g (o u) -> p g o u", u=2), in_=ctp[b, h][:].rearrange("p k u o -> p k o u"))

        def cq(b, h):
            if h == 0:
                t_cq = work.tile([P, NG2 * P], U32, name="t_cq", align_bytes=64)
                t_cs = work.tile([P, NG2 * P], U8, name="t_cs", align_bytes=64)
                cqs[b] = (t_cq, t_cs)
            t_cq, t_cs = cqs[b]
            width = NG2 // HALVES[b]
            cols = slice(P * width * h, P * width * h + P * width)
            nc.vector.quantize_mx(out=t_cq[:, cols].bitcast(FP8X4), scales=t_cs[:, cols], in_=tct[b][:, width * h : width * h + width, :, :].rearrange("p g o t -> p (g o t)"))

        def lmm(b, h):
            t_cq, t_cs = cqs[b]
            if h == 0:
                low = ps_l.tile([P, R], F32, name="low")
                lows[b] = low
            low = lows[b]
            width = NG2 // HALVES[b]
            for g in range(width * h, width * h + width):
                nc.tensor.matmul_mx(
                    out=low[:],
                    lhsT=t_cq[:, P * g : P * g + P].bitcast(FP8X4),
                    lhsT_scale=t_cs[:, P * g : P * g + P],
                    rhs=words[:, g, :].bitcast(FP4X4),
                    rhs_scale=planes[:, g, :],
                    start=(g == 0),
                    stop=(g == NG2 - 1),
                )

        def on_g(b):
            return b < G_EPI

        def part(b, c):
            width = R // PARTS[b]
            return slice(width * c, width * c + width)

        def esq(b, c):
            if c == 0:
                t_sq = work.tile([P, R], F32, name="t_sq", bufs=1)
                ep[b, "sq"] = t_sq
            k = part(b, c)
            nc.scalar.activation(out=ep[b, "sq"][:, k], in_=lows[b][:, k], func=ACT.Square, scale=sqrt(0.1))

        def em(b, c):
            if c == 0:
                t_m = work.tile([P, R], F32, name="t_m", bufs=2)
                ep[b, "m"] = t_m
            k = part(b, c)
            nc.vector.scalar_tensor_tensor(out=ep[b, "m"][:, k], in0=lows[b][:, k], scalar=0.25, in1=mt[:, b, k], op0=ALU.mult, op1=ALU.add)

        def ev9(b, c):
            if b < 0:
                t_v9 = work.tile([P, R], F32, name="t_v9", bufs=1)
                nc.gpsimd.tensor_scalar(out=t_v9[:], in0=vt[:, b, :], scalar1=0.9, scalar2=0.0, op0=ALU.mult, op1=ALU.add)
                ep[b, "v9"] = t_v9

        def ev(b, c):
            if c == 0:
                t_v = work.tile([P, R], F32, name="t_v", bufs=2)
                ep[b, "v"] = t_v
            k = part(b, c)
            t_v = ep[b, "v"]
            if b < 0:
                nc.gpsimd.tensor_tensor(out=t_v[:, k], in0=ep[b, "v9"][:, k], in1=ep[b, "sq"][:, k], op=ALU.add)
            else:
                nc.vector.scalar_tensor_tensor(out=t_v[:, k], in0=vt[:, b, k], scalar=0.9, in1=ep[b, "sq"][:, k], op0=ALU.mult, op1=ALU.add)
            nc.sync.dma_start(out=out_1[P * b : P * b + P, k], in_=t_v[:, k])

        def emn(b, c):
            if c == 0:
                t_mn = work.tile([P, R], F32, name="t_mn", bufs=2)
                ep[b, "mn"] = t_mn
            k = part(b, c)
            t_mn = ep[b, "mn"]
            if on_g(b):
                nc.gpsimd.tensor_scalar(out=t_mn[:, k], in0=ep[b, "m"][:, k], scalar1=0.8, scalar2=0.0, op0=ALU.mult, op1=ALU.add)
            else:
                nc.scalar.activation(out=t_mn[:, k], in_=ep[b, "m"][:, k], func=ACT.Copy, scale=0.8)
            nc.sync.dma_start(out=out_0[P * b : P * b + P, k], in_=t_mn[:, k])

        def ers(b, c):
            if c == 0:
                t_rs = work.tile([P, R], F32, name="t_rs", bufs=2)
                ep[b, "rs"] = t_rs
            k = part(b, c)
            nc.scalar.activation(out=ep[b, "rs"][:, k], in_=ep[b, "v"][:, k], func=ACT.Abs_reciprocal_sqrt, scale=1.0 / 0.64)

        def est(b, c):
            k = part(b, c)
            t_st = ep[b, "rs"]
            eng = nc.gpsimd if on_g(b) else nc.vector
            eng.tensor_tensor(out=t_st[:, k], in0=ep[b, "m"][:, k], in1=t_st[:, k], op=ALU.mult)
            nc.sync.dma_start(out=out_2[P * b : P * b + P, k], in_=t_st[:, k])

        def late(k):
            if k == 0:
                nc.sync.dma_start(out=pc_rows[0:1, :], in_=precond.rearrange("(o n) -> o n", o=1))
                nc.sync.dma_start(out=lim_rows[0:NB, :], in_=limit.rearrange("(b p) -> b p", p=P))
            elif k == 1:
                nc.sync.dma_start(out=words[:], in_=proj_words.rearrange("g p n -> p g n"))
            elif k == 2:
                for q in range(4):
                    nc.sync.dma_start(out=planes[32 * q : 32 * q + 4, :, :].bitcast(I32), in_=proj_scales[:, 4 * q : 4 * q + 4, :].rearrange("g q n -> q g n").bitcast(I32))
            else:
                s = k - 3
                nc.sync.dma_start(out=mt[:, 4 * s : 4 * s + 4, :], in_=m_view[:, 4 * s : 4 * s + 4, :])
                nc.sync.dma_start(out=vt[:, 4 * s : 4 * s + 4, :], in_=v_view[:, 4 * s : 4 * s + 4, :])

        steps = {"load_x": load_x, "load_gate": load_gate, "load_dh": load_dh, "load_acc": load_acc, "late": late, "silu": silu, "dmul": dmul, "dq": dq, "widen": widen, "inter": inter, "xq": xq, "amm": amm, "add": add, "sqr": sqr, "vectors": vectors, "ars": ars, "clip": clip, "cmul": cmul, "tr": tr, "cpt": cpt, "cq": cq, "lmm": lmm, "esq": esq, "em": em, "ev9": ev9, "ev": ev, "emn": emn, "ers": ers, "est": est}
        for s in SEQ:
            steps[s[0]](*s[1:])
